import numpy as np
import ml_dtypes


def mxq(x, axis, fmt="e4m3"):
    dtype, down = {"e4m3": (ml_dtypes.float8_e4m3fn, 7), "e5m2": (ml_dtypes.float8_e5m2, 14)}[fmt]
    v = np.moveaxis(np.asarray(x, np.float32).astype(ml_dtypes.bfloat16).astype(np.float64), axis, -1)
    blocks = v.reshape(v.shape[:-1] + (-1, 32))
    amax = np.abs(blocks).max(-1, keepdims=True)
    byte = np.maximum(np.where(amax > 0, np.frexp(amax)[1] - 1 + 127, 0) - down, 1)
    scale = np.exp2(byte - 127.0)
    codes = (blocks / scale).astype(np.float32).astype(dtype).astype(np.float64)
    return np.moveaxis((codes * scale).reshape(v.shape), -1, axis)


WIDE = False


def mx_kscale(k):
    if not WIDE:
        return np.ones(k)
    levels = np.array([10, -10, 5, -5, 0])
    if k % 512:
        return np.exp2(np.random.permutation(np.resize(levels, k // 32))).repeat(32)
    a = np.empty((k // 512, 16))
    for p in range(k // 512):
        a[p, :8] = np.random.permutation(np.resize(levels, 8))
        for g in range(8):
            far = levels[np.abs(levels - a[p, g]) >= 10]
            a[p, g + 8] = far[np.random.randint(len(far))]
    return np.exp2(a.ravel()).repeat(32)


def f64(x):
    return np.asarray(x).astype(np.float64)


def striped(idx):
    return np.tile(idx.reshape(-1, 16).T, (8, 1)).astype(np.uint16)


def unstriped(offs):
    return offs[:16].T.reshape(-1).astype(np.int64)


def pack_weight(w):
    k, n = w.shape
    w = f64(np.asarray(w, np.float32).astype(ml_dtypes.bfloat16)).reshape(k // 32, 32, n)
    amax = np.abs(w).max(1)
    byte = np.clip(np.where(amax > 0, np.frexp(amax)[1] - 1 + 127 - 7, 1), 1, 254)
    scaled = (w * np.exp2(127.0 - byte)[:, None, :]).reshape(k, n).astype(np.float32)
    words = np.ascontiguousarray(scaled.reshape(k // 512, 128, 4, n).transpose(0, 1, 3, 2)).astype(ml_dtypes.float8_e4m3fn).view(np.uint8)
    return words, np.ascontiguousarray(byte.astype(np.uint8).reshape(k // 512, 16, n))


def unpack_weight(words, scales):
    g, p, n, _ = words.shape
    vals = np.ascontiguousarray(words).view(ml_dtypes.float8_e4m3fn).astype(np.float64) * np.repeat(np.exp2(scales.astype(np.float64) - 127.0), 8, axis=1)[..., None]
    return vals.transpose(0, 1, 3, 2).reshape(g * 512, n)


def relu(v):
    return np.maximum(v, 0.0)


K, T, S, H, D, G = 512, 2048, 512, 512, 4, 512


def setup_inputs():
    n = np.random.standard_normal
    s = mx_kscale(K)[:, None]
    u = mx_kscale(H)
    packed_xT = pack_weight(n((K, T)) * s)
    return {
        "x_words": packed_xT[0],
        "x_scales": packed_xT[1],
        "w1": (n((K, H)) / np.sqrt(K) / s * u).astype(np.float32),
        "w2": (n((H, G)) / np.sqrt(H) / u[:, None]).astype(np.float32),
        "w3": (n((H, G)) / np.sqrt(H) / u[:, None]).astype(np.float32),
        "disc": (np.random.uniform(0.0, 0.99, (S, 1))).astype(np.float32),
        "rew": (n((S, 1))).astype(np.float32),
        "offs": striped(np.random.permutation(T)[:S]),
    }


def reference(x_words, x_scales, w1, w2, w3, disc, rew, offs):
    xq = unpack_weight(x_words, x_scales)[:, unstriped(offs)]
    h = relu(mxq(f64(w1), 0, "e4m3").T @ xq)
    hq = mxq(h, 0, "e4m3")
    w2q = mxq(f64(w2), 0, "e4m3")
    qa = hq.T @ w2q
    w3q = mxq(f64(w3), 0, "e4m3")
    qb = hq.T @ w3q
    qq = np.minimum(qa, qb)
    ee = np.exp(2.0 * qq)
    l = np.log(ee.reshape(len(ee), -1, D).sum(axis=2))
    return f64(disc) * (0.5 * l) + f64(rew)

@@ -1,0 +1,199 @@
+from contextlib import ExitStack
+
+import concourse.mybir as mybir
+
+K, T, S, H, D, G = 512, 2048, 512, 512, 4, 512
+FLOPS = 2 * S * H * (K + 2 * G)
+
+F32 = mybir.dt.float32
+BF16 = mybir.dt.bfloat16
+I32 = mybir.dt.int32
+U32 = mybir.dt.uint32
+U16 = mybir.dt.uint16
+U8 = mybir.dt.uint8
+FP8X4 = mybir.dt.float8_e4m3fn_x4
+ALU = mybir.AluOpType
+ACT = mybir.ActivationFunctionType
+
+P = 128
+PACK = 4
+HALF = 256
+V = G // D
+VH = HALF // D
+
+
+def tile_picked_ysoftq_lse_p_kernel(tc, x_words, x_scales, w1, w2, w3, disc, rew, offs, out):
+    nc = tc.nc
+    with ExitStack() as ctx:
+        keep = ctx.enter_context(tc.tile_pool(name="keep", bufs=1))
+        psum = ctx.enter_context(tc.psum_pool(name="psum", bufs=8))
+
+        def sb(name, shape, dtype):
+            return keep.tile(shape, dtype, name=name, align_bytes=64)
+
+        def bank():
+            return psum.tile([P, 512], F32, name="bank")
+
+        offsets = keep.tile([P, S // 16], U16, name="offsets")
+        xs = sb("xs", [P, T], U8)
+        xw = sb("xw", [P, T], I32)
+        w1_raw = sb("w1_raw", [P, PACK, H], F32)
+        warm = sb("warm", [P, 2], F32)
+
+        nc.vector.memset(xs[:].bitcast(I32), 0)
+        nc.gpsimd.memset(warm[:, 0:1], 0.0)
+        nc.scalar.activation(warm[:, 1:2], warm[:, 0:1], ACT.Exp)
+
+        for c in range(2):
+            nc.sync.dma_start(w1_raw[:, 2 * c : 2 * c + 2, :], w1.rearrange("(p j) c -> p j c", j=PACK)[:, 2 * c : 2 * c + 2, :])
+        nc.sync.dma_start(offsets[:], offs)
+        for q in range(4):
+            nc.sync.dma_start(xs[32 * q : 32 * q + 4, :].bitcast(I32), x_scales[0, 4 * q : 4 * q + 4, :].bitcast(I32))
+        nc.sync.dma_start(xw[:], x_words[0].rearrange("p n t -> p (n t)").bitcast(I32))
+        raw = {}
+        for c in range(2):
+            for i, w in enumerate((w2, w3)):
+                raw[i, c] = sb(f"raw{i}{c}", [P, PACK, HALF], F32)
+                nc.sync.dma_start(raw[i, c][:], w.rearrange("(p j) c -> p j c", j=PACK)[:, :, c * HALF : (c + 1) * HALF])
+        disc_sb = sb("disc_sb", [P, 4], F32)
+        rew_sb = sb("rew_sb", [P, 4], F32)
+        with nc.allow_non_contiguous_dma(reason="one value for each transition"):
+            nc.sync.dma_start(disc_sb[:], disc.rearrange("(s p) o -> p (s o)", p=P))
+            nc.sync.dma_start(rew_sb[:], rew.rearrange("(s p) o -> p (s o)", p=P))
+
+        xs_g = sb("xs_g", [P, S], U8)
+        nc.vector.tensor_copy(xs_g[:], xs[:].indirect(offsets[:]))
+
+        w1_bf = sb("w1_bf", [P, PACK, P, PACK], BF16)
+        for c, copy in enumerate((nc.vector.tensor_copy, nc.scalar.copy)):
+            copy(w1_bf[:, :, c * 64 : (c + 1) * 64, :].rearrange("p i m j -> p m i j"), w1_raw[:, :, c * HALF : (c + 1) * HALF].rearrange("p j (m i) -> p m i j", i=PACK))
+        w1_c = sb("w1_c", [P, H], U32)
+        w1_s = sb("w1_s", [P, H], U8)
+        nc.vector.quantize_mx(w1_c[:].bitcast(FP8X4), w1_s[:], w1_bf[:].rearrange("p i m j -> p (i m j)"))
+
+        xw_g = []
+        for half in range(2):
+            g = sb(f"xw_g{half}", [P, HALF], U32)
+            nc.vector.tensor_copy(g[:], xw[:].bitcast(U32).indirect(offsets[:, 16 * half : 16 * (half + 1)]))
+            xw_g.append(g)
+
+        h_bf = [sb(f"h_bf{tp}", [P, 2, P, PACK], BF16) for tp in range(2)]
+        for tt in range(4):
+            hb = bank()
+            cols = slice((tt % 2) * P, (tt % 2 + 1) * P)
+            for i in range(PACK):
+                ch = slice(i * P, (i + 1) * P)
+                nc.tensor.matmul_mx(hb[:, ch], lhsT=w1_c[:, ch].bitcast(FP8X4), lhsT_scale=w1_s[:, ch],
+                                    rhs=xw_g[tt // 2][:, cols].bitcast(FP8X4), rhs_scale=xs_g[:, tt * P : (tt + 1) * P],
+                                    start=True, stop=True)
+            nc.scalar.activation(h_bf[tt // 2][:, tt % 2, :, :], hb[:].rearrange("p (i n) -> p n i", i=PACK), ACT.Relu)
+
+        w_bf, w_c, w_s, h_c, h_s = {}, {}, {}, {}, {}
+
+        def cast_w(i, c, on_scalar):
+            w_bf[i, c] = sb(f"w_bf{i}{c}", [P, HALF, PACK], BF16)
+            dst = w_bf[i, c][:].rearrange("p (n e) j -> p n j e", e=4)
+            src = raw[i, c][:].rearrange("p j (n e) -> p n j e", e=4)
+            if on_scalar:
+                nc.vector.tensor_copy(dst[:, :42], src[:, :42])
+                nc.scalar.copy(dst[:, 42:], src[:, 42:])
+            else:
+                nc.vector.tensor_copy(dst, src)
+
+        def quant_w(i, c):
+            w_c[i, c] = sb(f"w_c{i}{c}", [P, HALF], U32)
+            w_s[i, c] = sb(f"w_s{i}{c}", [P, HALF], U8)
+            nc.vector.quantize_mx(w_c[i, c][:].bitcast(FP8X4), w_s[i, c][:], w_bf[i, c][:].rearrange("p n j -> p (n j)"))
+
+        def quant_h(tt):
+            h_c[tt] = sb(f"h_c{tt}", [P, HALF], U32)
+            h_s[tt] = sb(f"h_s{tt}", [P, HALF], U8)
+            nc.vector.quantize_mx(h_c[tt][:].bitcast(FP8X4), h_s[tt][:], h_bf[tt][:].rearrange("p s n j -> p (s n j)"))
+
+        cast_w(0, 0, False)
+        quant_w(0, 0)
+        cast_w(1, 0, False)
+        quant_h(0)
+        quant_w(1, 0)
+        quant_h(1)
+
+        top = [sb(f"top{tp}", [P, 2, V], F32) for tp in range(2)]
+        tot = [sb(f"tot{tp}", [P, 2, V], F32) for tp in range(2)]
+        qq, m2, dl, ee, qa_bank, qb_bank, qa_sb = {}, {}, {}, {}, {}, {}, {}
+
+        def dmajor(ap):
+            return ap.rearrange("p (g d) -> p d g", d=D)
+
+        def products(c, tp):
+            qa_bank[c, tp] = bank()
+            qb_bank[c, tp] = bank()
+            for i, dst in enumerate((qa_bank[c, tp], qb_bank[c, tp])):
+                for s in range(2):
+                    rows = slice(s * P, (s + 1) * P)
+                    nc.tensor.matmul_mx(dst[:, s * HALF : (s + 1) * HALF], lhsT=h_c[tp][:, rows].bitcast(FP8X4), lhsT_scale=h_s[tp][:, rows],
+                                        rhs=w_c[i, c][:].bitcast(FP8X4), rhs_scale=w_s[i, c][:], start=True, stop=True)
+            qa_sb[c, tp] = sb(f"qa{c}{tp}", [P, D, P], F32)
+            nc.scalar.copy(qa_sb[c, tp][:], dmajor(qa_bank[c, tp][:]))
+
+        def smaller(c, tp):
+            qq[c, tp] = sb(f"qq{c}{tp}", [P, D, P], F32)
+            nc.vector.tensor_tensor(qq[c, tp][:], dmajor(qb_bank[c, tp][:]), qa_sb[c, tp][:], ALU.min)
+
+        def part(tiles, c, tp):
+            return tiles[tp][:, :, c * VH : (c + 1) * VH]
+
+        def pairs(src, name, op):
+            t = sb(name, [P, 2, P], F32)
+            nc.vector.tensor_tensor(t[:], src[:, 0:2, :], src[:, 2:4, :], op)
+            return t
+
+        def last(dst, t, op):
+            nc.vector.tensor_tensor(dst, t[:, 0, :].rearrange("p (s v) -> p s v", s=2), t[:, 1, :].rearrange("p (s v) -> p s v", s=2), op)
+
+        def shift(c, tp):
+            dl[c, tp] = sb(f"dl{c}{tp}", [P, D, P], F32)
+            nc.vector.tensor_tensor(dl[c, tp][:].rearrange("p d (s v) -> p d s v", s=2), qq[c, tp][:].rearrange("p d (s v) -> p d s v", s=2),
+                                    part(top, c, tp).unsqueeze(1).to_broadcast([P, D, 2, VH]), ALU.subtract)
+            ee[c, tp] = sb(f"ee{c}{tp}", [P, D, P], F32)
+            nc.scalar.activation(ee[c, tp][:], dl[c, tp][:], ACT.Exp, scale=2.0)
+
+        for c in range(2):
+            for tp in range(2):
+                products(c, tp)
+            if c == 0:
+                cast_w(0, 1, True)
+                cast_w(1, 1, True)
+            for tp in range(2):
+                smaller(c, tp)
+            if c == 0:
+                quant_w(0, 1)
+            for tp in range(2):
+                m2[c, tp] = pairs(qq[c, tp], f"m2{c}{tp}", ALU.max)
+            if c == 0:
+                quant_w(1, 1)
+            for tp in range(2):
+                last(part(top, c, tp), m2[c, tp], ALU.max)
+            for tp in range(2):
+                shift(c, tp)
+
+        half_disc = sb("half_disc", [P, 4], F32)
+        nc.vector.tensor_scalar(half_disc[:], disc_sb[:], 0.5, None, ALU.mult)
+        s2 = {}
+        base = [sb(f"base{tp}", [P, 2, V], F32) for tp in range(2)]
+        for c in range(2):
+            for tp in range(2):
+                s2[c, tp] = pairs(ee[c, tp], f"s2{c}{tp}", ALU.add)
+                if c == 1:
+                    for s in range(2):
+                        tt = 2 * tp + s
+                        nc.vector.tensor_scalar(base[tp][:, s, :], top[tp][:, s, :], disc_sb[:, tt : tt + 1], rew_sb[:, tt : tt + 1], ALU.mult, ALU.add)
+            for tp in range(2):
+                last(part(tot, c, tp), s2[c, tp], ALU.add)
+
+        logs = dl[1, 1]
+        for tt in range(4):
+            tp, s = divmod(tt, 2)
+            nc.scalar.activation(logs[:, tt, :], tot[tp][:, s, :], ACT.Ln)
+            res = sb(f"res{tt}", [P, V], F32)
+            nc.vector.scalar_tensor_tensor(res[:], logs[:, tt, :], half_disc[:, tt : tt + 1], base[tp][:, s, :], ALU.mult, ALU.add)
+            nc.sync.dma_start(out[tt * P : (tt + 1) * P, :], res[:])

@@ -13,6 +13,7 @@ U16 = mybir.dt.uint16
 U8 = mybir.dt.uint8
 FP8X4 = mybir.dt.float8_e4m3fn_x4
 ALU = mybir.AluOpType
+AX = mybir.AxisListType.X
 ACT = mybir.ActivationFunctionType
 
 P = 128
@@ -28,8 +29,8 @@ def tile_picked_ysoftq_lse_p_kernel(tc, x_words, x_scales, w1, w2, w3, disc, rew
         keep = ctx.enter_context(tc.tile_pool(name="keep", bufs=1))
         psum = ctx.enter_context(tc.psum_pool(name="psum", bufs=8))
 
-        def sb(name, shape, dtype):
-            return keep.tile(shape, dtype, name=name, align_bytes=64)
+        def sb(name, shape, dtype, tag=None):
+            return keep.tile(shape, dtype, name=name, tag=tag or name, align_bytes=64)
 
         def bank():
             return psum.tile([P, 512], F32, name="bank")
@@ -37,7 +38,7 @@ def tile_picked_ysoftq_lse_p_kernel(tc, x_words, x_scales, w1, w2, w3, disc, rew
         offsets = keep.tile([P, S // 16], U16, name="offsets")
         xs = sb("xs", [P, T], U8)
         xw = sb("xw", [P, T], I32)
-        w1_raw = sb("w1_raw", [P, PACK, H], F32)
+        w1_raw = [sb(f"w1_raw{c}", [P, PACK, HALF], F32) for c in range(2)]
         warm = sb("warm", [P, 2], F32)
 
         nc.vector.memset(xs[:].bitcast(I32), 0)
@@ -45,11 +46,12 @@ def tile_picked_ysoftq_lse_p_kernel(tc, x_words, x_scales, w1, w2, w3, disc, rew
         nc.scalar.activation(warm[:, 1:2], warm[:, 0:1], ACT.Exp)
 
         for c in range(2):
-            nc.sync.dma_start(w1_raw[:, 2 * c : 2 * c + 2, :], w1.rearrange("(p j) c -> p j c", j=PACK)[:, 2 * c : 2 * c + 2, :])
+            nc.sync.dma_start(w1_raw[c][:], w1.rearrange("(p j) c -> p j c", j=PACK)[:, :, c * HALF : (c + 1) * HALF])
         nc.sync.dma_start(offsets[:], offs)
+        x_flat = x_words[0].rearrange("p n t -> p (n t)").bitcast(I32)
         for q in range(4):
             nc.sync.dma_start(xs[32 * q : 32 * q + 4, :].bitcast(I32), x_scales[0, 4 * q : 4 * q + 4, :].bitcast(I32))
-        nc.sync.dma_start(xw[:], x_words[0].rearrange("p n t -> p (n t)").bitcast(I32))
+        nc.sync.dma_start(xw[:], x_flat)
         raw = {}
         for c in range(2):
             for i, w in enumerate((w2, w3)):
@@ -65,8 +67,8 @@ def tile_picked_ysoftq_lse_p_kernel(tc, x_words, x_scales, w1, w2, w3, disc, rew
         nc.vector.tensor_copy(xs_g[:], xs[:].indirect(offsets[:]))
 
         w1_bf = sb("w1_bf", [P, PACK, P, PACK], BF16)
-        for c, copy in enumerate((nc.vector.tensor_copy, nc.scalar.copy)):
-            copy(w1_bf[:, :, c * 64 : (c + 1) * 64, :].rearrange("p i m j -> p m i j"), w1_raw[:, :, c * HALF : (c + 1) * HALF].rearrange("p j (m i) -> p m i j", i=PACK))
+        for c in range(2):
+            nc.vector.tensor_copy(w1_bf[:, :, c * 64 : (c + 1) * 64, :].rearrange("p i m j -> p m i j"), w1_raw[c][:].rearrange("p j (m i) -> p m i j", i=PACK))
         w1_c = sb("w1_c", [P, H], U32)
         w1_s = sb("w1_s", [P, H], U8)
         nc.vector.quantize_mx(w1_c[:].bitcast(FP8X4), w1_s[:], w1_bf[:].rearrange("p i m j -> p (i m j)"))
@@ -91,12 +93,11 @@ def tile_picked_ysoftq_lse_p_kernel(tc, x_words, x_scales, w1, w2, w3, disc, rew
         w_bf, w_c, w_s, h_c, h_s = {}, {}, {}, {}, {}
 
         def cast_w(i, c, on_scalar):
-            w_bf[i, c] = sb(f"w_bf{i}{c}", [P, HALF, PACK], BF16)
+            w_bf[i, c] = sb(f"w_bf{i}{c}", [P, HALF, PACK], BF16, tag=f"h_bf{i}" if c else None)
             dst = w_bf[i, c][:].rearrange("p (n e) j -> p n j e", e=4)
             src = raw[i, c][:].rearrange("p j (n e) -> p n j e", e=4)
             if on_scalar:
-                nc.vector.tensor_copy(dst[:, :42], src[:, :42])
-                nc.scalar.copy(dst[:, 42:], src[:, 42:])
+                nc.scalar.copy(dst, src)
             else:
                 nc.vector.tensor_copy(dst, src)
 
@@ -116,13 +117,14 @@ def tile_picked_ysoftq_lse_p_kernel(tc, x_words, x_scales, w1, w2, w3, disc, rew
         quant_h(0)
         quant_w(1, 0)
         quant_h(1)
+        cast_w(0, 1, True)
+        cast_w(1, 1, False)
+        quant_w(0, 1)
+        quant_w(1, 1)
 
         top = [sb(f"top{tp}", [P, 2, V], F32) for tp in range(2)]
         tot = [sb(f"tot{tp}", [P, 2, V], F32) for tp in range(2)]
         qq, m2, dl, ee, qa_bank, qb_bank, qa_sb = {}, {}, {}, {}, {}, {}, {}
-
-        def dmajor(ap):
-            return ap.rearrange("p (g d) -> p d g", d=D)
 
         def products(c, tp):
             qa_bank[c, tp] = bank()
@@ -132,68 +134,53 @@ def tile_picked_ysoftq_lse_p_kernel(tc, x_words, x_scales, w1, w2, w3, disc, rew
                     rows = slice(s * P, (s + 1) * P)
                     nc.tensor.matmul_mx(dst[:, s * HALF : (s + 1) * HALF], lhsT=h_c[tp][:, rows].bitcast(FP8X4), lhsT_scale=h_s[tp][:, rows],
                                         rhs=w_c[i, c][:].bitcast(FP8X4), rhs_scale=w_s[i, c][:], start=True, stop=True)
-            qa_sb[c, tp] = sb(f"qa{c}{tp}", [P, D, P], F32)
-            nc.scalar.copy(qa_sb[c, tp][:], dmajor(qa_bank[c, tp][:]))
+            qa_sb[c, tp] = sb(f"qa{c}{tp}", [P, 512], F32)
+            nc.scalar.copy(qa_sb[c, tp][:], qa_bank[c, tp][:])
+
+        def groups(t):
+            return t[:].rearrange("p (s v d) -> p s v d", s=2, d=D)
 
         def smaller(c, tp):
-            qq[c, tp] = sb(f"qq{c}{tp}", [P, D, P], F32)
-            nc.vector.tensor_tensor(qq[c, tp][:], dmajor(qb_bank[c, tp][:]), qa_sb[c, tp][:], ALU.min)
+            qq[c, tp] = sb(f"qq{c}{tp}", [P, 512], F32)
+            nc.vector.tensor_tensor(qq[c, tp][:], qb_bank[c, tp][:], qa_sb[c, tp][:], ALU.min)
 
         def part(tiles, c, tp):
             return tiles[tp][:, :, c * VH : (c + 1) * VH]
 
-        def pairs(src, name, op):
-            t = sb(name, [P, 2, P], F32)
-            nc.vector.tensor_tensor(t[:], src[:, 0:2, :], src[:, 2:4, :], op)
-            return t
-
-        def last(dst, t, op):
-            nc.vector.tensor_tensor(dst, t[:, 0, :].rearrange("p (s v) -> p s v", s=2), t[:, 1, :].rearrange("p (s v) -> p s v", s=2), op)
-
         def shift(c, tp):
-            dl[c, tp] = sb(f"dl{c}{tp}", [P, D, P], F32)
-            nc.vector.tensor_tensor(dl[c, tp][:].rearrange("p d (s v) -> p d s v", s=2), qq[c, tp][:].rearrange("p d (s v) -> p d s v", s=2),
-                                    part(top, c, tp).unsqueeze(1).to_broadcast([P, D, 2, VH]), ALU.subtract)
-            ee[c, tp] = sb(f"ee{c}{tp}", [P, D, P], F32)
+            dl[c, tp] = sb(f"dl{c}{tp}", [P, 512], F32)
+            eng = nc.gpsimd if c == 0 else nc.vector
+            eng.tensor_tensor(groups(dl[c, tp]), groups(qq[c, tp]), part(top, c, tp).unsqueeze(3).to_broadcast([P, 2, VH, D]), ALU.subtract)
+            ee[c, tp] = sb(f"ee{c}{tp}", [P, 512], F32)
             nc.scalar.activation(ee[c, tp][:], dl[c, tp][:], ACT.Exp, scale=2.0)
 
         for c in range(2):
             for tp in range(2):
                 products(c, tp)
-            if c == 0:
-                cast_w(0, 1, True)
-                cast_w(1, 1, True)
             for tp in range(2):
                 smaller(c, tp)
-            if c == 0:
-                quant_w(0, 1)
             for tp in range(2):
-                m2[c, tp] = pairs(qq[c, tp], f"m2{c}{tp}", ALU.max)
-            if c == 0:
-                quant_w(1, 1)
-            for tp in range(2):
-                last(part(top, c, tp), m2[c, tp], ALU.max)
+                nc.vector.tensor_reduce(part(top, c, tp), groups(qq[c, tp]), AX, ALU.max)
             for tp in range(2):
                 shift(c, tp)
 
-        half_disc = sb("half_disc", [P, 4], F32)
-        nc.vector.tensor_scalar(half_disc[:], disc_sb[:], 0.5, None, ALU.mult)
-        s2 = {}
+        half_disc = qq[1, 1]
+        nc.vector.tensor_scalar(half_disc[:, 0:4], disc_sb[:], 0.5, None, ALU.mult)
         base = [sb(f"base{tp}", [P, 2, V], F32) for tp in range(2)]
         for c in range(2):
             for tp in range(2):
-                s2[c, tp] = pairs(ee[c, tp], f"s2{c}{tp}", ALU.add)
+                nc.vector.tensor_reduce(part(tot, c, tp), groups(ee[c, tp]), AX, ALU.add)
                 if c == 1:
                     for s in range(2):
                         tt = 2 * tp + s
                         nc.vector.tensor_scalar(base[tp][:, s, :], top[tp][:, s, :], disc_sb[:, tt : tt + 1], rew_sb[:, tt : tt + 1], ALU.mult, ALU.add)
-            for tp in range(2):
-                last(part(tot, c, tp), s2[c, tp], ALU.add)
 
-        logs = dl[1, 1]
-        for tt in range(4):
-            tp, s = divmod(tt, 2)
-            nc.scalar.activation(logs[:, tt, :], tot[tp][:, s, :], ACT.Ln)
-            res = sb(f"res{tt}", [P, V], F32)
-            nc.vector.scalar_tensor_tensor(res[:], logs[:, tt, :], half_disc[:, tt : tt + 1], base[tp][:, s, :], ALU.mult, ALU.add)
-            nc.sync.dma_start(out[tt * P : (tt + 1) * P, :], res[:])
+        logs = dl[1, 1][:].rearrange("p (t v) -> p t v", t=4)
+        for tp in range(2):
+            for c in range(2):
+                nc.scalar.activation(logs[:, 2 * tp : 2 * tp + 2, c * VH : (c + 1) * VH], part(tot, c, tp), ACT.Ln)
+            for s in range(2):
+                tt = 2 * tp + s
+                res = sb(f"res{tt}", [P, V], F32)
+                nc.vector.scalar_tensor_tensor(res[:], logs[:, tt, :], half_disc[:, tt : tt + 1], base[tp][:, s, :], ALU.mult, ALU.add)
+                nc.sync.dma_start(out[tt * P : (tt + 1) * P, :], res[:])

@@ -39,11 +39,8 @@ def tile_picked_ysoftq_lse_p_kernel(tc, x_words, x_scales, w1, w2, w3, disc, rew
         xs = sb("xs", [P, T], U8)
         xw = sb("xw", [P, T], I32)
         w1_raw = [sb(f"w1_raw{c}", [P, PACK, HALF], F32) for c in range(2)]
-        warm = sb("warm", [P, 2], F32)
 
         nc.vector.memset(xs[:].bitcast(I32), 0)
-        nc.gpsimd.memset(warm[:, 0:1], 0.0)
-        nc.scalar.activation(warm[:, 1:2], warm[:, 0:1], ACT.Exp)
 
         for c in range(2):
             nc.sync.dma_start(w1_raw[c][:], w1.rearrange("(p j) c -> p j c", j=PACK)[:, :, c * HALF : (c + 1) * HALF])

@@ -89,10 +89,11 @@ def tile_picked_ysoftq_lse_p_kernel(tc, x_words, x_scales, w1, w2, w3, disc, rew
 
         w_bf, w_c, w_s, h_c, h_s = {}, {}, {}, {}, {}
 
-        def cast_w(i, c, on_scalar):
-            w_bf[i, c] = sb(f"w_bf{i}{c}", [P, HALF, PACK], BF16, tag=f"h_bf{i}" if c else None)
-            dst = w_bf[i, c][:].rearrange("p (n e) j -> p n j e", e=4)
-            src = raw[i, c][:].rearrange("p j (n e) -> p n j e", e=4)
+        def cast_w(i, c, lo, hi, on_scalar):
+            if (i, c) not in w_bf:
+                w_bf[i, c] = sb(f"w_bf{i}{c}", [P, HALF, PACK], BF16)
+            dst = w_bf[i, c][:, lo:hi, :].rearrange("p (n e) j -> p n j e", e=4)
+            src = raw[i, c][:, :, lo:hi].rearrange("p j (n e) -> p n j e", e=4)
             if on_scalar:
                 nc.scalar.copy(dst, src)
             else:
@@ -108,20 +109,12 @@ def tile_picked_ysoftq_lse_p_kernel(tc, x_words, x_scales, w1, w2, w3, disc, rew
             h_s[tt] = sb(f"h_s{tt}", [P, HALF], U8)
             nc.vector.quantize_mx(h_c[tt][:].bitcast(FP8X4), h_s[tt][:], h_bf[tt][:].rearrange("p s n j -> p (s n j)"))
 
-        cast_w(0, 0, False)
-        quant_w(0, 0)
-        cast_w(1, 0, False)
-        quant_h(0)
-        quant_w(1, 0)
-        quant_h(1)
-        cast_w(0, 1, True)
-        cast_w(1, 1, False)
-        quant_w(0, 1)
-        quant_w(1, 1)
-
         top = [sb(f"top{tp}", [P, 2, V], F32) for tp in range(2)]
-        tot = [sb(f"tot{tp}", [P, 2, V], F32) for tp in range(2)]
-        qq, m2, dl, ee, qa_bank, qb_bank, qa_sb = {}, {}, {}, {}, {}, {}, {}
+        tot = [sb(f"tot{tp}", [P, 2 * V], F32) for tp in range(2)]
+        ee = [sb(f"ee{tp}", [P, 2, G], F32) for tp in range(2)]
+        base = [sb("base0", [P, 2, V], F32), top[1]]
+        qq, dl, qa_bank, qb_bank, qa_sb = {}, {}, {}, {}, {}
+        BOTH = slice(0, 2)
 
         def products(c, tp):
             qa_bank[c, tp] = bank()
@@ -144,40 +137,80 @@ def tile_picked_ysoftq_lse_p_kernel(tc, x_words, x_scales, w1, w2, w3, disc, rew
         def part(tiles, c, tp):
             return tiles[tp][:, :, c * VH : (c + 1) * VH]
 
-        def shift(c, tp):
-            dl[c, tp] = sb(f"dl{c}{tp}", [P, 512], F32)
-            eng = nc.gpsimd if c == 0 else nc.vector
-            eng.tensor_tensor(groups(dl[c, tp]), groups(qq[c, tp]), part(top, c, tp).unsqueeze(3).to_broadcast([P, 2, VH, D]), ALU.subtract)
-            ee[c, tp] = sb(f"ee{c}{tp}", [P, 512], F32)
-            nc.scalar.activation(ee[c, tp][:], dl[c, tp][:], ACT.Exp, scale=2.0)
+        def largest(c, tp, ss):
+            nc.vector.tensor_reduce(part(top, c, tp)[:, ss, :], groups(qq[c, tp])[:, ss], AX, ALU.max)
 
-        for c in range(2):
-            for tp in range(2):
-                products(c, tp)
-            for tp in range(2):
-                smaller(c, tp)
-            for tp in range(2):
-                nc.vector.tensor_reduce(part(top, c, tp), groups(qq[c, tp]), AX, ALU.max)
-            for tp in range(2):
-                shift(c, tp)
+        def shift(c, tp, ss, eng):
+            if (c, tp) not in dl:
+                dl[c, tp] = sb(f"dl{c}{tp}", [P, 512], F32)
+            n = ss.stop - ss.start
+            eng.tensor_tensor(groups(dl[c, tp])[:, ss], groups(qq[c, tp])[:, ss], part(top, c, tp)[:, ss, :].unsqueeze(3).to_broadcast([P, n, VH, D]), ALU.subtract)
+            nc.scalar.activation(ee[tp][:, ss, c * HALF : (c + 1) * HALF], dl[c, tp][:].rearrange("p (s n) -> p s n", s=2)[:, ss, :], ACT.Exp, scale=2.0)
 
-        half_disc = qq[1, 1]
-        nc.vector.tensor_scalar(half_disc[:, 0:4], disc_sb[:], 0.5, None, ALU.mult)
-        base = [sb(f"base{tp}", [P, 2, V], F32) for tp in range(2)]
-        for c in range(2):
-            for tp in range(2):
-                nc.vector.tensor_reduce(part(tot, c, tp), groups(ee[c, tp]), AX, ALU.add)
-                if c == 1:
-                    for s in range(2):
-                        tt = 2 * tp + s
-                        nc.vector.tensor_scalar(base[tp][:, s, :], top[tp][:, s, :], disc_sb[:, tt : tt + 1], rew_sb[:, tt : tt + 1], ALU.mult, ALU.add)
-
-        logs = dl[1, 1][:].rearrange("p (t v) -> p t v", t=4)
-        for tp in range(2):
-            for c in range(2):
-                nc.scalar.activation(logs[:, 2 * tp : 2 * tp + 2, c * VH : (c + 1) * VH], part(tot, c, tp), ACT.Ln)
+        def make_base(tp, on_scalar):
             for s in range(2):
                 tt = 2 * tp + s
-                res = sb(f"res{tt}", [P, V], F32)
-                nc.vector.scalar_tensor_tensor(res[:], logs[:, tt, :], half_disc[:, tt : tt + 1], base[tp][:, s, :], ALU.mult, ALU.add)
-                nc.sync.dma_start(out[tt * P : (tt + 1) * P, :], res[:])
+                if on_scalar:
+                    nc.scalar.activation(base[tp][:, s, :], top[tp][:, s, :], ACT.Identity, bias=rew_sb[:, tt : tt + 1], scale=disc_sb[:, tt : tt + 1])
+                else:
+                    nc.vector.tensor_scalar(base[tp][:, s, :], top[tp][:, s, :], disc_sb[:, tt : tt + 1], rew_sb[:, tt : tt + 1], ALU.mult, ALU.add)
+
+        SPLIT = 160
+        EARLY = 16
+        cast_w(0, 0, 0, HALF, False)
+        quant_w(0, 0)
+        cast_w(1, 0, 0, HALF, False)
+        quant_h(0)
+        quant_w(1, 0)
+        products(0, 0)
+        cast_w(0, 1, 0, HALF, False)
+        quant_h(1)
+        products(0, 1)
+        cast_w(1, 1, 0, SPLIT, True)
+        cast_w(1, 1, SPLIT, HALF, False)
+        quant_w(0, 1)
+        smaller(0, 0)
+        quant_w(1, 1)
+        products(1, 0)
+        products(1, 1)
+        half_disc = sb("half_disc", [P, 4], F32)
+        nc.scalar.mul(half_disc[:], disc_sb[:], 0.5)
+        largest(0, 0, BOTH)
+        shift(0, 0, BOTH, nc.gpsimd)
+        smaller(0, 1)
+        smaller(1, 0)
+        largest(0, 1, BOTH)
+        shift(0, 1, BOTH, nc.gpsimd)
+        smaller(1, 1)
+        largest(1, 0, BOTH)
+        make_base(0, True)
+        largest(1, 1, BOTH)
+        flat = [ee[tp][:].rearrange("p s (v d) -> p (s v) d", d=D) for tp in range(2)]
+        nc.vector.tensor_reduce(tot[0][:, 0:EARLY], flat[0][:, 0:EARLY, :], AX, ALU.add)
+        for tp in range(2):
+            for s in range(2):
+                shift(1, tp, slice(s, s + 1), nc.vector)
+
+        pair = [qq[1, 1][:].rearrange("p (n d) -> p n d", d=2), qq[1, 0][:].rearrange("p (n d) -> p n d", d=2)]
+
+        def add_pairs(tp, lo):
+            nc.vector.tensor_tensor(pair[tp][:, lo:, :], flat[tp][:, lo:, 0:2], flat[tp][:, lo:, 2:4], ALU.add)
+
+        def add_last(tp, lo):
+            nc.vector.tensor_tensor(tot[tp][:, lo:], pair[tp][:, lo:, 0], pair[tp][:, lo:, 1], ALU.add)
+
+        add_pairs(0, EARLY)
+        make_base(1, False)
+        add_last(0, EARLY)
+        add_pairs(1, 0)
+        add_last(1, 0)
+
+        logs = dl[1, 1][:].rearrange("p (t v) -> p t v", t=4)
+        nc.scalar.activation(logs[:, 2, 0:EARLY], tot[0][:, 0:EARLY], ACT.Ln)
+        for tt in range(4):
+            tp, s = divmod(tt, 2)
+            lo = EARLY if tt == 0 else 0
+            nc.scalar.activation(logs[:, (tt + 2) % 4, lo:], tot[tp][:, s * V + lo : (s + 1) * V], ACT.Ln)
+            res = sb(f"res{tt}", [P, V], F32)
+            nc.vector.scalar_tensor_tensor(res[:], logs[:, (tt + 2) % 4, :], half_disc[:, tt : tt + 1], base[tp][:, s, :], ALU.mult, ALU.add)
+            nc.sync.dma_start(out[tt * P : (tt + 1) * P, :], res[:])

@@ -27,31 +27,40 @@ def tile_picked_ysoftq_lse_p_kernel(tc, x_words, x_scales, w1, w2, w3, disc, rew
     nc = tc.nc
     with ExitStack() as ctx:
         keep = ctx.enter_context(tc.tile_pool(name="keep", bufs=1))
-        psum = ctx.enter_context(tc.psum_pool(name="psum", bufs=8))
+        psum = ctx.enter_context(tc.psum_pool(name="psum", bufs=1))
 
         def sb(name, shape, dtype, tag=None):
             return keep.tile(shape, dtype, name=name, tag=tag or name, align_bytes=64)
 
-        def bank():
-            return psum.tile([P, 512], F32, name="bank")
+        def bank(b):
+            return psum.tile([P, 512], F32, name=f"bank{b}")
 
         offsets = keep.tile([P, S // 16], U16, name="offsets")
         xs = sb("xs", [P, T], U8)
         xw = sb("xw", [P, T], I32)
-        w1_raw = [sb(f"w1_raw{c}", [P, PACK, HALF], F32) for c in range(2)]
+        w1_raw = sb("w1_raw", [P, PACK, H], F32)
 
         nc.vector.memset(xs[:].bitcast(I32), 0)
+        early = sb("early", [P, 16], F32)
+        nc.gpsimd.memset(early[:, 0:8], 0.0)
+        nc.scalar.activation(early[:, 8:9], early[:, 0:1], ACT.Exp)
 
-        for c in range(2):
-            nc.sync.dma_start(w1_raw[c][:], w1.rearrange("(p j) c -> p j c", j=PACK)[:, :, c * HALF : (c + 1) * HALF])
+        w1_rows = w1.rearrange("(p j) c -> p j c", j=PACK)
+        nc.sync.dma_start(w1_raw[:, 0:2, :], w1_rows[:, 0:2, :])
         nc.sync.dma_start(offsets[:], offs)
         x_flat = x_words[0].rearrange("p n t -> p (n t)").bitcast(I32)
-        for q in range(4):
-            nc.sync.dma_start(xs[32 * q : 32 * q + 4, :].bitcast(I32), x_scales[0, 4 * q : 4 * q + 4, :].bitcast(I32))
+        for r in range(4):
+            nc.sync.dma_start(xs[r:P:32, :].bitcast(I32), x_scales[0, r:16:4, :].bitcast(I32))
+        nc.sync.dma_start(w1_raw[:, 2:4, :], w1_rows[:, 2:4, :])
         nc.sync.dma_start(xw[:], x_flat)
         raw = {}
         for c in range(2):
             for i, w in enumerate((w2, w3)):
+                if (i, c) == (1, 1):
+                    raw[i, c] = [sb(f"raw11_{u}", [P, PACK, P], F32) for u in range(2)]
+                    for u in range(2):
+                        nc.sync.dma_start(raw[i, c][u][:], w.rearrange("(p j) c -> p j c", j=PACK)[:, :, HALF + u * P : HALF + (u + 1) * P])
+                    continue
                 raw[i, c] = sb(f"raw{i}{c}", [P, PACK, HALF], F32)
                 nc.sync.dma_start(raw[i, c][:], w.rearrange("(p j) c -> p j c", j=PACK)[:, :, c * HALF : (c + 1) * HALF])
         disc_sb = sb("disc_sb", [P, 4], F32)
@@ -64,11 +73,15 @@ def tile_picked_ysoftq_lse_p_kernel(tc, x_words, x_scales, w1, w2, w3, disc, rew
         nc.vector.tensor_copy(xs_g[:], xs[:].indirect(offsets[:]))
 
         w1_bf = sb("w1_bf", [P, PACK, P, PACK], BF16)
-        for c in range(2):
-            nc.vector.tensor_copy(w1_bf[:, :, c * 64 : (c + 1) * 64, :].rearrange("p i m j -> p m i j"), w1_raw[c][:].rearrange("p j (m i) -> p m i j", i=PACK))
+        for lo, hi, copy in ((0, 84, nc.vector.tensor_copy), (84, P, nc.scalar.copy)):
+            copy(w1_bf[:, :, lo:hi, :].rearrange("p i m j -> p m i j"), w1_raw[:, :, PACK * lo : PACK * hi].rearrange("p j (m i) -> p m i j", i=PACK))
         w1_c = sb("w1_c", [P, H], U32)
         w1_s = sb("w1_s", [P, H], U8)
         nc.vector.quantize_mx(w1_c[:].bitcast(FP8X4), w1_s[:], w1_bf[:].rearrange("p i m j -> p (i m j)"))
+
+        warm = bank(7)
+        for r in range(2):
+            nc.tensor.matmul_mx(warm[:], lhsT=w1_c[:, 0:P].bitcast(FP8X4), lhsT_scale=w1_s[:, 0:P], rhs=w1_c[:].bitcast(FP8X4), rhs_scale=w1_s[:], start=True, stop=True)
 
         xw_g = []
         for half in range(2):
@@ -78,7 +91,7 @@ def tile_picked_ysoftq_lse_p_kernel(tc, x_words, x_scales, w1, w2, w3, disc, rew
 
         h_bf = [sb(f"h_bf{tp}", [P, 2, P, PACK], BF16) for tp in range(2)]
         for tt in range(4):
-            hb = bank()
+            hb = bank(tt)
             cols = slice((tt % 2) * P, (tt % 2 + 1) * P)
             for i in range(PACK):
                 ch = slice(i * P, (i + 1) * P)
@@ -93,7 +106,7 @@ def tile_picked_ysoftq_lse_p_kernel(tc, x_words, x_scales, w1, w2, w3, disc, rew
             if (i, c) not in w_bf:
                 w_bf[i, c] = sb(f"w_bf{i}{c}", [P, HALF, PACK], BF16)
             dst = w_bf[i, c][:, lo:hi, :].rearrange("p (n e) j -> p n j e", e=4)
-            src = raw[i, c][:, :, lo:hi].rearrange("p j (n e) -> p n j e", e=4)
+            src = (raw[i, c][lo // P][:] if (i, c) == (1, 1) else raw[i, c][:, :, lo:hi]).rearrange("p j (n e) -> p n j e", e=4)
             if on_scalar:
                 nc.scalar.copy(dst, src)
             else:
@@ -105,7 +118,7 @@ def tile_picked_ysoftq_lse_p_kernel(tc, x_words, x_scales, w1, w2, w3, disc, rew
             nc.vector.quantize_mx(w_c[i, c][:].bitcast(FP8X4), w_s[i, c][:], w_bf[i, c][:].rearrange("p n j -> p (n j)"))
 
         def quant_h(tt):
-            h_c[tt] = sb(f"h_c{tt}", [P, HALF], U32)
+            h_c[tt] = sb(f"h_c{tt}", [P, HALF], U32, tag="raw01" if tt else "raw10")
             h_s[tt] = sb(f"h_s{tt}", [P, HALF], U8)
             nc.vector.quantize_mx(h_c[tt][:].bitcast(FP8X4), h_s[tt][:], h_bf[tt][:].rearrange("p s n j -> p (s n j)"))
 
@@ -115,24 +128,28 @@ def tile_picked_ysoftq_lse_p_kernel(tc, x_words, x_scales, w1, w2, w3, disc, rew
         base = [sb("base0", [P, 2, V], F32), top[1]]
         qq, dl, qa_bank, qb_bank, qa_sb = {}, {}, {}, {}, {}
         BOTH = slice(0, 2)
+        qa_late = []
 
         def products(c, tp):
-            qa_bank[c, tp] = bank()
-            qb_bank[c, tp] = bank()
+            qa_bank[c, tp] = bank(4 * (1 - c) + 2 * tp)
+            qb_bank[c, tp] = bank(4 * (1 - c) + 2 * tp + 1)
             for i, dst in enumerate((qa_bank[c, tp], qb_bank[c, tp])):
                 for s in range(2):
                     rows = slice(s * P, (s + 1) * P)
                     nc.tensor.matmul_mx(dst[:, s * HALF : (s + 1) * HALF], lhsT=h_c[tp][:, rows].bitcast(FP8X4), lhsT_scale=h_s[tp][:, rows],
                                         rhs=w_c[i, c][:].bitcast(FP8X4), rhs_scale=w_s[i, c][:], start=True, stop=True)
-            qa_sb[c, tp] = sb(f"qa{c}{tp}", [P, 512], F32)
-            nc.scalar.copy(qa_sb[c, tp][:], qa_bank[c, tp][:])
+            if (c, tp) == (0, 1):
+                qa_late.append(sb("qa_late", [P, 3 * 512], F32, tag="raw11_1"))
+            n = 2 * c + tp - 1
+            qa_sb[c, tp] = qa_late[0][:, n * 512 : (n + 1) * 512] if n >= 0 else sb("qa_first", [P, 512], F32)[:]
+            nc.scalar.copy(qa_sb[c, tp], qa_bank[c, tp][:])
 
         def groups(t):
             return t[:].rearrange("p (s v d) -> p s v d", s=2, d=D)
 
         def smaller(c, tp):
-            qq[c, tp] = sb(f"qq{c}{tp}", [P, 512], F32)
-            nc.vector.tensor_tensor(qq[c, tp][:], qb_bank[c, tp][:], qa_sb[c, tp][:], ALU.min)
+            qq[c, tp] = sb(f"qq{c}{tp}", [P, 512], F32, tag="raw11_0" if (c, tp) == (0, 0) else None)
+            nc.vector.tensor_tensor(qq[c, tp][:], qb_bank[c, tp][:], qa_sb[c, tp], ALU.min)
 
         def part(tiles, c, tp):
             return tiles[tp][:, :, c * VH : (c + 1) * VH]
@@ -142,7 +159,7 @@ def tile_picked_ysoftq_lse_p_kernel(tc, x_words, x_scales, w1, w2, w3, disc, rew
 
         def shift(c, tp, ss, eng):
             if (c, tp) not in dl:
-                dl[c, tp] = sb(f"dl{c}{tp}", [P, 512], F32)
+                dl[c, tp] = sb(f"dl{c}{tp}", [P, 512], F32, tag="w_bf11" if (c, tp) == (0, 0) else None)
             n = ss.stop - ss.start
             eng.tensor_tensor(groups(dl[c, tp])[:, ss], groups(qq[c, tp])[:, ss], part(top, c, tp)[:, ss, :].unsqueeze(3).to_broadcast([P, n, VH, D]), ALU.subtract)
             nc.scalar.activation(ee[tp][:, ss, c * HALF : (c + 1) * HALF], dl[c, tp][:].rearrange("p (s n) -> p s n", s=2)[:, ss, :], ACT.Exp, scale=2.0)
@@ -155,19 +172,18 @@ def tile_picked_ysoftq_lse_p_kernel(tc, x_words, x_scales, w1, w2, w3, disc, rew
                 else:
                     nc.vector.tensor_scalar(base[tp][:, s, :], top[tp][:, s, :], disc_sb[:, tt : tt + 1], rew_sb[:, tt : tt + 1], ALU.mult, ALU.add)
 
-        SPLIT = 160
         EARLY = 16
         cast_w(0, 0, 0, HALF, False)
         quant_w(0, 0)
         cast_w(1, 0, 0, HALF, False)
-        quant_h(0)
         quant_w(1, 0)
+        quant_h(0)
         products(0, 0)
         cast_w(0, 1, 0, HALF, False)
         quant_h(1)
+        cast_w(1, 1, 0, P, False)
+        cast_w(1, 1, P, HALF, True)
         products(0, 1)
-        cast_w(1, 1, 0, SPLIT, True)
-        cast_w(1, 1, SPLIT, HALF, False)
         quant_w(0, 1)
         smaller(0, 0)
         quant_w(1, 1)
@@ -181,15 +197,16 @@ def tile_picked_ysoftq_lse_p_kernel(tc, x_words, x_scales, w1, w2, w3, disc, rew
         smaller(1, 0)
         largest(0, 1, BOTH)
         shift(0, 1, BOTH, nc.gpsimd)
-        smaller(1, 1)
         largest(1, 0, BOTH)
+        smaller(1, 1)
         make_base(0, True)
-        largest(1, 1, BOTH)
+        shift(1, 0, BOTH, nc.vector)
         flat = [ee[tp][:].rearrange("p s (v d) -> p (s v) d", d=D) for tp in range(2)]
         nc.vector.tensor_reduce(tot[0][:, 0:EARLY], flat[0][:, 0:EARLY, :], AX, ALU.add)
-        for tp in range(2):
-            for s in range(2):
-                shift(1, tp, slice(s, s + 1), nc.vector)
+        for s in range(2):
+            largest(1, 1, slice(s, s + 1))
+        for s in range(2):
+            shift(1, 1, slice(s, s + 1), nc.vector)
 
         pair = [qq[1, 1][:].rearrange("p (n d) -> p n d", d=2), qq[1, 0][:].rearrange("p (n d) -> p n d", d=2)]
 

@@ -1,6 +1,7 @@
 from contextlib import ExitStack
 
 import concourse.mybir as mybir
+from concourse.masks import make_identity
 
 K, T, S, H, D, G = 512, 2048, 512, 512, 4, 512
 FLOPS = 2 * S * H * (K + 2 * G)
@@ -44,6 +45,8 @@ def tile_picked_ysoftq_lse_p_kernel(tc, x_words, x_scales, w1, w2, w3, disc, rew
         early = sb("early", [P, 16], F32)
         nc.gpsimd.memset(early[:, 0:8], 0.0)
         nc.scalar.activation(early[:, 8:9], early[:, 0:1], ACT.Exp)
+        ident = sb("ident", [P, P], F32)
+        make_identity(nc, ident[:])
 
         w1_rows = w1.rearrange("(p j) c -> p j c", j=PACK)
         nc.sync.dma_start(w1_raw[:, 0:2, :], w1_rows[:, 0:2, :])
@@ -122,13 +125,16 @@ def tile_picked_ysoftq_lse_p_kernel(tc, x_words, x_scales, w1, w2, w3, disc, rew
             h_s[tt] = sb(f"h_s{tt}", [P, HALF], U8)
             nc.vector.quantize_mx(h_c[tt][:].bitcast(FP8X4), h_s[tt][:], h_bf[tt][:].rearrange("p s n j -> p (s n j)"))
 
-        top = [sb(f"top{tp}", [P, 2, V], F32) for tp in range(2)]
-        tot = [sb(f"tot{tp}", [P, 2 * V], F32) for tp in range(2)]
-        ee = [sb(f"ee{tp}", [P, 2, G], F32) for tp in range(2)]
-        base = [sb("base0", [P, 2, V], F32), top[1]]
-        qq, dl, qa_bank, qb_bank, qa_sb = {}, {}, {}, {}, {}
-        BOTH = slice(0, 2)
+        LAST = (1, 1)
+        neg_top = [sb(f"neg_top{tp}", [P, 2, 2, VH], F32) for tp in range(2)]
+        qq, qa_bank, qb_bank, qa_sb = {}, {}, {}, {}
         qa_late = []
+
+        def read(bank_ap, c, tp):
+            return bank_ap if (c, tp) == LAST else bank_ap.rearrange("p (n d) -> p d n", d=D)
+
+        def laid(tile_ap, c, tp):
+            return tile_ap if (c, tp) == LAST else tile_ap.rearrange("p (d n) -> p d n", d=D)
 
         def products(c, tp):
             qa_bank[c, tp] = bank(4 * (1 - c) + 2 * tp)
@@ -142,37 +148,48 @@ def tile_picked_ysoftq_lse_p_kernel(tc, x_words, x_scales, w1, w2, w3, disc, rew
                 qa_late.append(sb("qa_late", [P, 3 * 512], F32, tag="raw11_1"))
             n = 2 * c + tp - 1
             qa_sb[c, tp] = qa_late[0][:, n * 512 : (n + 1) * 512] if n >= 0 else sb("qa_first", [P, 512], F32)[:]
-            nc.scalar.copy(qa_sb[c, tp], qa_bank[c, tp][:])
-
-        def groups(t):
-            return t[:].rearrange("p (s v d) -> p s v d", s=2, d=D)
+            nc.scalar.copy(laid(qa_sb[c, tp], c, tp), read(qa_bank[c, tp][:], c, tp))
 
         def smaller(c, tp):
             qq[c, tp] = sb(f"qq{c}{tp}", [P, 512], F32, tag="raw11_0" if (c, tp) == (0, 0) else None)
-            nc.vector.tensor_tensor(qq[c, tp][:], qb_bank[c, tp][:], qa_sb[c, tp], ALU.min)
+            nc.vector.tensor_tensor(laid(qq[c, tp][:], c, tp), read(qb_bank[c, tp][:], c, tp), laid(qa_sb[c, tp], c, tp), ALU.min)
 
-        def part(tiles, c, tp):
-            return tiles[tp][:, :, c * VH : (c + 1) * VH]
+        def shift_of(c, tp):
+            return neg_top[tp][:, c].rearrange("p s v -> p (s v)")
 
-        def largest(c, tp, ss):
-            nc.vector.tensor_reduce(part(top, c, tp)[:, ss, :], groups(qq[c, tp])[:, ss], AX, ALU.max)
+        def largest(c, tp):
+            nc.vector.tensor_reduce(shift_of(c, tp), qq[c, tp][:].rearrange("p (d n) -> p n d", d=D), AX, ALU.max, negate=True)
 
-        def shift(c, tp, ss, eng):
-            if (c, tp) not in dl:
-                dl[c, tp] = sb(f"dl{c}{tp}", [P, 512], F32, tag="w_bf11" if (c, tp) == (0, 0) else None)
-            n = ss.stop - ss.start
-            eng.tensor_tensor(groups(dl[c, tp])[:, ss], groups(qq[c, tp])[:, ss], part(top, c, tp)[:, ss, :].unsqueeze(3).to_broadcast([P, n, VH, D]), ALU.subtract)
-            nc.scalar.activation(ee[tp][:, ss, c * HALF : (c + 1) * HALF], dl[c, tp][:].rearrange("p (s n) -> p s n", s=2)[:, ss, :], ACT.Exp, scale=2.0)
+        def turn(dst, src, start, stop):
+            nc.tensor.matmul(dst, lhsT=src, rhs=ident[:], start=start, stop=stop, is_transpose=True)
 
-        def make_base(tp, on_scalar):
-            for s in range(2):
-                tt = 2 * tp + s
-                if on_scalar:
-                    nc.scalar.activation(base[tp][:, s, :], top[tp][:, s, :], ACT.Identity, bias=rew_sb[:, tt : tt + 1], scale=disc_sb[:, tt : tt + 1])
-                else:
-                    nc.vector.tensor_scalar(base[tp][:, s, :], top[tp][:, s, :], disc_sb[:, tt : tt + 1], rew_sb[:, tt : tt + 1], ALU.mult, ALU.add)
+        ee = {}
 
-        EARLY = 16
+        def shift_in_one_bank(c, tp, b):
+            ee[c, tp] = sb(f"ee{c}{tp}", [P, 512], F32)
+            diff = bank(b)
+            for d in range(D):
+                cols = slice(d * P, (d + 1) * P)
+                turn(diff[:, cols], qq[c, tp][:, cols], True, False)
+                turn(diff[:, cols], shift_of(c, tp), False, True)
+            nc.scalar.activation(ee[c, tp][:], diff[:], ACT.Exp, scale=2.0)
+
+        def open_four(c, tp, banks):
+            diffs = [bank(b) for b in banks]
+            for d in range(D):
+                turn(diffs[d][:, 0:P], qq[c, tp][:, d * P : (d + 1) * P], True, False)
+            return diffs
+
+        def close_four(c, tp, diffs):
+            ee[c, tp] = sb(f"ee{c}{tp}", [P, 512], F32)
+            for d in range(D):
+                turn(diffs[d][:, 0:P], shift_of(c, tp), False, True)
+                nc.scalar.activation(ee[c, tp][:, d * P : (d + 1) * P], diffs[d][:, 0:P], ACT.Exp, scale=2.0)
+
+        def sum_back(c, tp, dst):
+            for d in range(D):
+                turn(dst, ee[c, tp][:, d * P : (d + 1) * P], d == 0, d == D - 1)
+
         cast_w(0, 0, 0, HALF, False)
         quant_w(0, 0)
         cast_w(1, 0, 0, HALF, False)
@@ -191,43 +208,54 @@ def tile_picked_ysoftq_lse_p_kernel(tc, x_words, x_scales, w1, w2, w3, disc, rew
         products(1, 1)
         half_disc = sb("half_disc", [P, 4], F32)
         nc.scalar.mul(half_disc[:], disc_sb[:], 0.5)
-        largest(0, 0, BOTH)
-        shift(0, 0, BOTH, nc.gpsimd)
+        neg_disc = sb("neg_disc", [P, 4], F32)
+        nc.scalar.mul(neg_disc[:], disc_sb[:], -1.0)
+        largest(0, 0)
+        shift_in_one_bank(0, 0, 4)
         smaller(0, 1)
         smaller(1, 0)
-        largest(0, 1, BOTH)
-        shift(0, 1, BOTH, nc.gpsimd)
-        largest(1, 0, BOTH)
+        largest(0, 1)
+        shift_in_one_bank(0, 1, 5)
+        largest(1, 0)
+        diffs = open_four(1, 0, (6, 7, 0, 1))
+        close_four(1, 0, diffs)
         smaller(1, 1)
-        make_base(0, True)
-        shift(1, 0, BOTH, nc.vector)
-        flat = [ee[tp][:].rearrange("p s (v d) -> p (s v) d", d=D) for tp in range(2)]
-        nc.vector.tensor_reduce(tot[0][:, 0:EARLY], flat[0][:, 0:EARLY, :], AX, ALU.add)
+
+        last_q = qq[LAST][:].rearrange("p (s v d) -> p s v d", s=2, d=D)
+        last_d = sb("last_d", [P, 2, VH, D], F32)
+        last_e = sb("last_e", [P, 2, VH, D], F32)
         for s in range(2):
-            largest(1, 1, slice(s, s + 1))
+            nc.vector.tensor_reduce(neg_top[1][:, 1, s, :], last_q[:, s], AX, ALU.max, negate=True)
         for s in range(2):
-            shift(1, 1, slice(s, s + 1), nc.vector)
+            nc.vector.tensor_tensor(last_d[:, s], last_q[:, s], neg_top[1][:, 1, s, :].unsqueeze(2).to_broadcast([P, VH, D]), ALU.add)
+            nc.scalar.activation(last_e[:, s], last_d[:, s], ACT.Exp, scale=2.0)
 
-        pair = [qq[1, 1][:].rearrange("p (n d) -> p n d", d=2), qq[1, 0][:].rearrange("p (n d) -> p n d", d=2)]
+        sums_first = bank(2)
+        sums_second = bank(4)
+        sum_back(0, 0, sums_first[:, 0:P])
+        sum_back(0, 1, sums_second[:, 0:P])
+        sum_back(1, 0, sums_first[:, P : 2 * P])
 
-        def add_pairs(tp, lo):
-            nc.vector.tensor_tensor(pair[tp][:, lo:, :], flat[tp][:, lo:, 0:2], flat[tp][:, lo:, 2:4], ALU.add)
-
-        def add_last(tp, lo):
-            nc.vector.tensor_tensor(tot[tp][:, lo:], pair[tp][:, lo:, 0], pair[tp][:, lo:, 1], ALU.add)
-
-        add_pairs(0, EARLY)
-        make_base(1, False)
-        add_last(0, EARLY)
-        add_pairs(1, 0)
-        add_last(1, 0)
-
-        logs = dl[1, 1][:].rearrange("p (t v) -> p t v", t=4)
-        nc.scalar.activation(logs[:, 2, 0:EARLY], tot[0][:, 0:EARLY], ACT.Ln)
+        base = [qq[LAST][:, HALF:].rearrange("p (c s v) -> p c s v", c=2, s=2), neg_top[1]]
         for tt in range(4):
             tp, s = divmod(tt, 2)
-            lo = EARLY if tt == 0 else 0
-            nc.scalar.activation(logs[:, (tt + 2) % 4, lo:], tot[tp][:, s * V + lo : (s + 1) * V], ACT.Ln)
-            res = sb(f"res{tt}", [P, V], F32)
-            nc.vector.scalar_tensor_tensor(res[:], logs[:, (tt + 2) % 4, :], half_disc[:, tt : tt + 1], base[tp][:, s, :], ALU.mult, ALU.add)
-            nc.sync.dma_start(out[tt * P : (tt + 1) * P, :], res[:])
+            nc.vector.tensor_scalar(base[tp][:, :, s, :], neg_top[tp][:, :, s, :], neg_disc[:, tt : tt + 1], rew_sb[:, tt : tt + 1], ALU.mult, ALU.add)
+        sums_last = sb("sums_last", [P, 2 * VH], F32)
+        nc.vector.tensor_reduce(sums_last[:], last_e[:].rearrange("p s v d -> p (s v) d"), AX, ALU.add)
+
+        logs = [t[:, 1].rearrange("p v d -> p (v d)").rearrange("p (c s v) -> p c s v", c=2, s=2) for t in (last_e, last_d)]
+
+        def finish(tt):
+            tp, s = divmod(tt, 2)
+            res = sb(f"res{tt}", [P, 2, VH], F32)
+            nc.vector.scalar_tensor_tensor(res[:], logs[tp][:, :, s, :], half_disc[:, tt : tt + 1], base[tp][:, :, s, :], ALU.mult, ALU.add)
+            nc.sync.dma_start(out[tt * P : (tt + 1) * P, :], res[:].rearrange("p c v -> p (c v)"))
+
+        nc.scalar.activation(logs[1][:, 0].rearrange("p s v -> p (s v)"), sums_second[:, 0:P], ACT.Ln)
+        nc.scalar.activation(logs[1][:, 1].rearrange("p s v -> p (s v)"), sums_last[:], ACT.Ln)
+        finish(2)
+        finish(3)
+        first = sums_first[:, 0 : 2 * P].rearrange("p (c s v) -> p c s v", c=2, s=2)
+        for s in range(2):
+            nc.scalar.activation(logs[0][:, :, s, :], first[:, :, s, :], ACT.Ln)
+            finish(s)

@@ -15,6 +15,7 @@ U8 = mybir.dt.uint8
 FP8X4 = mybir.dt.float8_e4m3fn_x4
 ALU = mybir.AluOpType
 AX = mybir.AxisListType.X
+AXY = mybir.AxisListType.XY
 ACT = mybir.ActivationFunctionType
 
 P = 128
@@ -28,10 +29,14 @@ def tile_picked_ysoftq_lse_p_kernel(tc, x_words, x_scales, w1, w2, w3, disc, rew
     nc = tc.nc
     with ExitStack() as ctx:
         keep = ctx.enter_context(tc.tile_pool(name="keep", bufs=1))
+        shared = ctx.enter_context(tc.tile_pool(name="shared", bufs=1))
         psum = ctx.enter_context(tc.psum_pool(name="psum", bufs=1))
 
         def sb(name, shape, dtype, tag=None):
             return keep.tile(shape, dtype, name=name, tag=tag or name, align_bytes=64)
+
+        def over(name, shape, dtype, offset):
+            return shared.tile(shape, dtype, name=name, offset=offset, align_bytes=64)
 
         def bank(b):
             return psum.tile([P, 512], F32, name=f"bank{b}")
@@ -64,7 +69,7 @@ def tile_picked_ysoftq_lse_p_kernel(tc, x_words, x_scales, w1, w2, w3, disc, rew
                     for u in range(2):
                         nc.sync.dma_start(raw[i, c][u][:], w.rearrange("(p j) c -> p j c", j=PACK)[:, :, HALF + u * P : HALF + (u + 1) * P])
                     continue
-                raw[i, c] = sb(f"raw{i}{c}", [P, PACK, HALF], F32)
+                raw[i, c] = over("raw01", [P, PACK, HALF], F32, 0) if (i, c) == (0, 1) else sb(f"raw{i}{c}", [P, PACK, HALF], F32)
                 nc.sync.dma_start(raw[i, c][:], w.rearrange("(p j) c -> p j c", j=PACK)[:, :, c * HALF : (c + 1) * HALF])
         disc_sb = sb("disc_sb", [P, 4], F32)
         rew_sb = sb("rew_sb", [P, 4], F32)
@@ -115,122 +120,143 @@ def tile_picked_ysoftq_lse_p_kernel(tc, x_words, x_scales, w1, w2, w3, disc, rew
             else:
                 nc.vector.tensor_copy(dst, src)
 
-        def quant_w(i, c):
-            w_c[i, c] = sb(f"w_c{i}{c}", [P, HALF], U32)
-            w_s[i, c] = sb(f"w_s{i}{c}", [P, HALF], U8)
-            nc.vector.quantize_mx(w_c[i, c][:].bitcast(FP8X4), w_s[i, c][:], w_bf[i, c][:].rearrange("p n j -> p (n j)"))
+        def quant_w(i, c, lo, hi):
+            if (i, c) not in w_c:
+                w_c[i, c] = sb(f"w_c{i}{c}", [P, HALF], U32)
+                w_s[i, c] = sb(f"w_s{i}{c}", [P, HALF], U8)
+            nc.vector.quantize_mx(w_c[i, c][:, lo:hi].bitcast(FP8X4), w_s[i, c][:, lo:hi], w_bf[i, c][:, lo:hi, :].rearrange("p n j -> p (n j)"))
 
-        def quant_h(tt):
-            h_c[tt] = sb(f"h_c{tt}", [P, HALF], U32, tag="raw01" if tt else "raw10")
-            h_s[tt] = sb(f"h_s{tt}", [P, HALF], U8)
-            nc.vector.quantize_mx(h_c[tt][:].bitcast(FP8X4), h_s[tt][:], h_bf[tt][:].rearrange("p s n j -> p (s n j)"))
+        def quant_h(tp):
+            h_c[tp] = over("h_c1", [P, HALF], U32, 0) if tp else sb("h_c0", [P, HALF], U32, tag="raw10")
+            h_s[tp] = sb(f"h_s{tp}", [P, HALF], U8)
+            nc.vector.quantize_mx(h_c[tp][:].bitcast(FP8X4), h_s[tp][:], h_bf[tp][:].rearrange("p s n j -> p (s n j)"))
 
         LAST = (1, 1)
-        neg_top = [sb(f"neg_top{tp}", [P, 2, 2, VH], F32) for tp in range(2)]
-        qq, qa_bank, qb_bank, qa_sb = {}, {}, {}, {}
-        qa_late = []
+        qq, q_bank, qa_sb, neg_top, ee, diff = {}, {}, {}, {}, {}, {}
 
         def read(bank_ap, c, tp):
-            return bank_ap if (c, tp) == LAST else bank_ap.rearrange("p (n d) -> p d n", d=D)
+            return bank_ap if (c, tp) == LAST else bank_ap.rearrange("p (n a b) -> p a n b", a=2, b=2)
 
         def laid(tile_ap, c, tp):
-            return tile_ap if (c, tp) == LAST else tile_ap.rearrange("p (d n) -> p d n", d=D)
+            return tile_ap if (c, tp) == LAST else tile_ap.rearrange("p (a n b) -> p a n b", a=2, b=2)
 
-        def products(c, tp):
-            qa_bank[c, tp] = bank(4 * (1 - c) + 2 * tp)
-            qb_bank[c, tp] = bank(4 * (1 - c) + 2 * tp + 1)
-            for i, dst in enumerate((qa_bank[c, tp], qb_bank[c, tp])):
-                for s in range(2):
-                    rows = slice(s * P, (s + 1) * P)
-                    nc.tensor.matmul_mx(dst[:, s * HALF : (s + 1) * HALF], lhsT=h_c[tp][:, rows].bitcast(FP8X4), lhsT_scale=h_s[tp][:, rows],
-                                        rhs=w_c[i, c][:].bitcast(FP8X4), rhs_scale=w_s[i, c][:], start=True, stop=True)
-            if (c, tp) == (0, 1):
-                qa_late.append(sb("qa_late", [P, 3 * 512], F32, tag="raw11_1"))
-            n = 2 * c + tp - 1
-            qa_sb[c, tp] = qa_late[0][:, n * 512 : (n + 1) * 512] if n >= 0 else sb("qa_first", [P, 512], F32)[:]
-            nc.scalar.copy(laid(qa_sb[c, tp], c, tp), read(qa_bank[c, tp][:], c, tp))
+        def product(i, c, tp):
+            q_bank[i, c, tp] = bank(4 * (1 - c) + 2 * tp + i)
+            for s in range(2):
+                rows = slice(s * P, (s + 1) * P)
+                nc.tensor.matmul_mx(q_bank[i, c, tp][:, s * HALF : (s + 1) * HALF], lhsT=h_c[tp][:, rows].bitcast(FP8X4), lhsT_scale=h_s[tp][:, rows],
+                                    rhs=w_c[i, c][:].bitcast(FP8X4), rhs_scale=w_s[i, c][:], start=True, stop=True)
 
-        def smaller(c, tp):
-            qq[c, tp] = sb(f"qq{c}{tp}", [P, 512], F32, tag="raw11_0" if (c, tp) == (0, 0) else None)
-            nc.vector.tensor_tensor(laid(qq[c, tp][:], c, tp), read(qb_bank[c, tp][:], c, tp), laid(qa_sb[c, tp], c, tp), ALU.min)
+        def first_out(c, tp, dst):
+            qa_sb[c, tp] = dst
+            nc.scalar.copy(laid(dst, c, tp), read(q_bank[0, c, tp][:], c, tp))
+
+        def smaller(c, tp, dst, lo=0, hi=P):
+            qq[c, tp] = dst
+            nc.vector.tensor_tensor(laid(dst, c, tp)[:, :, lo:hi], read(q_bank[1, c, tp][:], c, tp)[:, :, lo:hi], laid(qa_sb[c, tp], c, tp)[:, :, lo:hi], ALU.min)
 
         def shift_of(c, tp):
             return neg_top[tp][:, c].rearrange("p s v -> p (s v)")
 
-        def largest(c, tp):
-            nc.vector.tensor_reduce(shift_of(c, tp), qq[c, tp][:].rearrange("p (d n) -> p n d", d=D), AX, ALU.max, negate=True)
+        def largest(c, tp, lo=0, hi=P):
+            nc.vector.tensor_reduce(shift_of(c, tp)[:, lo:hi], qq[c, tp].rearrange("p (a n b) -> p n a b", a=2, b=2)[:, lo:hi], AXY, ALU.max, negate=True)
 
         def turn(dst, src, start, stop):
             nc.tensor.matmul(dst, lhsT=src, rhs=ident[:], start=start, stop=stop, is_transpose=True)
 
-        ee = {}
+        def open_values(c, tp, banks):
+            tiles = {b: bank(b) for b in sorted(set(banks))}
+            diff[c, tp] = [tiles[b] for b in banks]
+            for d in range(D):
+                a, b = divmod(d, 2)
+                turn(diff[c, tp][d][:, d * P : (d + 1) * P], qq[c, tp][:, a * HALF + b : (a + 1) * HALF : 2], d == 0 or len(tiles) == D, False)
 
-        def shift_in_one_bank(c, tp, b):
-            ee[c, tp] = sb(f"ee{c}{tp}", [P, 512], F32)
-            diff = bank(b)
+        def close_shift(c, tp, dst):
+            ee[c, tp] = dst
+            apart = (c, tp) == (1, 0)
             for d in range(D):
                 cols = slice(d * P, (d + 1) * P)
-                turn(diff[:, cols], qq[c, tp][:, cols], True, False)
-                turn(diff[:, cols], shift_of(c, tp), False, True)
-            nc.scalar.activation(ee[c, tp][:], diff[:], ACT.Exp, scale=2.0)
-
-        def open_four(c, tp, banks):
-            diffs = [bank(b) for b in banks]
-            for d in range(D):
-                turn(diffs[d][:, 0:P], qq[c, tp][:, d * P : (d + 1) * P], True, False)
-            return diffs
-
-        def close_four(c, tp, diffs):
-            ee[c, tp] = sb(f"ee{c}{tp}", [P, 512], F32)
-            for d in range(D):
-                turn(diffs[d][:, 0:P], shift_of(c, tp), False, True)
-                nc.scalar.activation(ee[c, tp][:, d * P : (d + 1) * P], diffs[d][:, 0:P], ACT.Exp, scale=2.0)
+                turn(diff[c, tp][d][:, cols], shift_of(c, tp), False, apart or d == D - 1)
+                if apart:
+                    nc.scalar.activation(dst[:, cols], diff[c, tp][d][:, cols], ACT.Exp, scale=2.0)
+            if not apart:
+                nc.scalar.activation(dst, diff[c, tp][0][:], ACT.Exp, scale=2.0)
 
         def sum_back(c, tp, dst):
             for d in range(D):
                 turn(dst, ee[c, tp][:, d * P : (d + 1) * P], d == 0, d == D - 1)
 
-        cast_w(0, 0, 0, HALF, False)
-        quant_w(0, 0)
-        cast_w(1, 0, 0, HALF, False)
-        quant_w(1, 0)
+        cast_w(0, 0, 0, P, False)
+        cast_w(0, 0, P, HALF, False)
+        quant_w(0, 0, 0, P)
+        quant_w(0, 0, P, HALF)
+        cast_w(1, 0, 0, P, False)
+        cast_w(1, 0, P, HALF, False)
+        quant_w(1, 0, 0, P)
         quant_h(0)
-        products(0, 0)
-        cast_w(0, 1, 0, HALF, False)
+        quant_w(1, 0, P, HALF)
+        product(0, 0, 0)
+        product(1, 0, 0)
+        first_out(0, 0, sb("qa00", [P, 512], F32)[:])
+        cast_w(0, 1, 0, P, False)
+        cast_w(0, 1, P, HALF, False)
+        quant_w(0, 1, 0, P)
         quant_h(1)
-        cast_w(1, 1, 0, P, False)
+        product(0, 0, 1)
+        product(1, 0, 1)
+        cast_w(1, 1, 0, P, True)
         cast_w(1, 1, P, HALF, True)
-        products(0, 1)
-        quant_w(0, 1)
-        smaller(0, 0)
-        quant_w(1, 1)
-        products(1, 0)
-        products(1, 1)
-        half_disc = sb("half_disc", [P, 4], F32)
-        nc.scalar.mul(half_disc[:], disc_sb[:], 0.5)
-        neg_disc = sb("neg_disc", [P, 4], F32)
-        nc.scalar.mul(neg_disc[:], disc_sb[:], -1.0)
-        largest(0, 0)
-        shift_in_one_bank(0, 0, 4)
-        smaller(0, 1)
-        smaller(1, 0)
+        late = sb("late", [P, 5, 512], F32, tag="raw11_1")
+        neg_top[0] = sb("neg_top0", [P, 2, 2, VH], F32)[:]
+        neg_top[1] = sb("neg_top1", [P, 2, 2, VH], F32)[:]
+        first_out(0, 1, late[:, 0])
+        quant_w(0, 1, P, HALF)
+        product(0, 1, 0)
+        product(0, 1, 1)
+        first_out(1, 0, late[:, 1])
+        first_out(1, 1, late[:, 2])
+        qq_first = over("qq00", [P, 512], F32, 4 * HALF)
+        smaller(0, 0, qq_first[:], 0, VH)
+        smaller(0, 0, qq_first[:], VH, P)
+        open_values(0, 0, [4] * D)
+        largest(0, 0, 0, VH)
+        largest(0, 0, VH, P)
+        quant_w(1, 1, 0, HALF)
+        product(1, 1, 0)
+        product(1, 1, 1)
+        close_shift(0, 0, late[:, 3])
+        smaller(0, 1, late[:, 4])
+        open_values(0, 1, [6] * D)
+        smaller(1, 0, sb("qq10", [P, 512], F32)[:])
         largest(0, 1)
-        shift_in_one_bank(0, 1, 5)
-        largest(1, 0)
-        diffs = open_four(1, 0, (6, 7, 0, 1))
-        close_four(1, 0, diffs)
-        smaller(1, 1)
+        close_shift(0, 1, sb("ee01", [P, 512], F32)[:])
+        open_values(1, 0, [0, 2, 7, 1])
 
+        half_disc = sb("half_disc", [P, 4], F32)
+        nc.gpsimd.tensor_scalar(half_disc[:], disc_sb[:], 0.5, 0.0, ALU.mult, ALU.add)
+        neg_disc = sb("neg_disc", [P, 4], F32)
+        nc.gpsimd.tensor_scalar(neg_disc[:], disc_sb[:], -1.0, 0.0, ALU.mult, ALU.add)
+
+        qq[LAST] = sb("qq11", [P, 512], F32)
         last_q = qq[LAST][:].rearrange("p (s v d) -> p s v d", s=2, d=D)
         last_d = sb("last_d", [P, 2, VH, D], F32)
         last_e = sb("last_e", [P, 2, VH, D], F32)
+
+        def smaller_last(s):
+            cols = slice(s * HALF, (s + 1) * HALF)
+            nc.vector.tensor_tensor(qq[LAST][:, cols], q_bank[1, 1, 1][:, cols], qa_sb[LAST][:, cols], ALU.min)
+
+        smaller_last(0)
+        largest(1, 0)
+        close_shift(1, 0, sb("ee10", [P, 512], F32)[:])
+        smaller_last(1)
         for s in range(2):
             nc.vector.tensor_reduce(neg_top[1][:, 1, s, :], last_q[:, s], AX, ALU.max, negate=True)
         for s in range(2):
             nc.vector.tensor_tensor(last_d[:, s], last_q[:, s], neg_top[1][:, 1, s, :].unsqueeze(2).to_broadcast([P, VH, D]), ALU.add)
             nc.scalar.activation(last_e[:, s], last_d[:, s], ACT.Exp, scale=2.0)
 
-        sums_first = bank(2)
+        sums_first = bank(5)
         sums_second = bank(4)
         sum_back(0, 0, sums_first[:, 0:P])
         sum_back(0, 1, sums_second[:, 0:P])
@@ -251,10 +277,10 @@ def tile_picked_ysoftq_lse_p_kernel(tc, x_words, x_scales, w1, w2, w3, disc, rew
             nc.vector.scalar_tensor_tensor(res[:], logs[tp][:, :, s, :], half_disc[:, tt : tt + 1], base[tp][:, :, s, :], ALU.mult, ALU.add)
             nc.sync.dma_start(out[tt * P : (tt + 1) * P, :], res[:].rearrange("p c v -> p (c v)"))
 
-        nc.scalar.activation(logs[1][:, 0].rearrange("p s v -> p (s v)"), sums_second[:, 0:P], ACT.Ln)
-        nc.scalar.activation(logs[1][:, 1].rearrange("p s v -> p (s v)"), sums_last[:], ACT.Ln)
-        finish(2)
-        finish(3)
+        for s in range(2):
+            nc.scalar.activation(logs[1][:, 0, s, :], sums_second[:, s * VH : (s + 1) * VH], ACT.Ln)
+            nc.scalar.activation(logs[1][:, 1, s, :], sums_last[:, s * VH : (s + 1) * VH], ACT.Ln)
+            finish(2 + s)
         first = sums_first[:, 0 : 2 * P].rearrange("p (c s v) -> p c s v", c=2, s=2)
         for s in range(2):
             nc.scalar.activation(logs[0][:, :, s, :], first[:, :, s, :], ACT.Ln)

@@ -64,10 +64,10 @@ def tile_picked_ysoftq_lse_p_kernel(tc, x_words, x_scales, w1, w2, w3, disc, rew
         raw = {}
         for c in range(2):
             for i, w in enumerate((w2, w3)):
-                if (i, c) == (1, 1):
-                    raw[i, c] = [sb(f"raw11_{u}", [P, PACK, P], F32) for u in range(2)]
+                if i == c:
+                    raw[i, c] = [sb(f"raw{i}{c}_{u}", [P, PACK, P], F32) for u in range(2)]
                     for u in range(2):
-                        nc.sync.dma_start(raw[i, c][u][:], w.rearrange("(p j) c -> p j c", j=PACK)[:, :, HALF + u * P : HALF + (u + 1) * P])
+                        nc.sync.dma_start(raw[i, c][u][:], w.rearrange("(p j) c -> p j c", j=PACK)[:, :, c * HALF + u * P : c * HALF + (u + 1) * P])
                     continue
                 raw[i, c] = over("raw01", [P, PACK, HALF], F32, 0) if (i, c) == (0, 1) else sb(f"raw{i}{c}", [P, PACK, HALF], F32)
                 nc.sync.dma_start(raw[i, c][:], w.rearrange("(p j) c -> p j c", j=PACK)[:, :, c * HALF : (c + 1) * HALF])
@@ -114,7 +114,7 @@ def tile_picked_ysoftq_lse_p_kernel(tc, x_words, x_scales, w1, w2, w3, disc, rew
             if (i, c) not in w_bf:
                 w_bf[i, c] = sb(f"w_bf{i}{c}", [P, HALF, PACK], BF16)
             dst = w_bf[i, c][:, lo:hi, :].rearrange("p (n e) j -> p n j e", e=4)
-            src = (raw[i, c][lo // P][:] if (i, c) == (1, 1) else raw[i, c][:, :, lo:hi]).rearrange("p j (n e) -> p n j e", e=4)
+            src = (raw[i, c][lo // P][:] if i == c else raw[i, c][:, :, lo:hi]).rearrange("p j (n e) -> p n j e", e=4)
             if on_scalar:
                 nc.scalar.copy(dst, src)
             else:
@@ -135,10 +135,10 @@ def tile_picked_ysoftq_lse_p_kernel(tc, x_words, x_scales, w1, w2, w3, disc, rew
         qq, q_bank, qa_sb, neg_top, ee, diff = {}, {}, {}, {}, {}, {}
 
         def read(bank_ap, c, tp):
-            return bank_ap if (c, tp) == LAST else bank_ap.rearrange("p (n a b) -> p a n b", a=2, b=2)
+            return bank_ap if c == tp else bank_ap.rearrange("p (n a b) -> p a n b", a=2, b=2)
 
         def laid(tile_ap, c, tp):
-            return tile_ap if (c, tp) == LAST else tile_ap.rearrange("p (a n b) -> p a n b", a=2, b=2)
+            return tile_ap if c == tp else tile_ap.rearrange("p (a n b) -> p a n b", a=2, b=2)
 
         def product(i, c, tp):
             q_bank[i, c, tp] = bank(4 * (1 - c) + 2 * tp + i)
@@ -158,8 +158,8 @@ def tile_picked_ysoftq_lse_p_kernel(tc, x_words, x_scales, w1, w2, w3, disc, rew
         def shift_of(c, tp):
             return neg_top[tp][:, c].rearrange("p s v -> p (s v)")
 
-        def largest(c, tp, lo=0, hi=P):
-            nc.vector.tensor_reduce(shift_of(c, tp)[:, lo:hi], qq[c, tp].rearrange("p (a n b) -> p n a b", a=2, b=2)[:, lo:hi], AXY, ALU.max, negate=True)
+        def largest(c, tp):
+            nc.vector.tensor_reduce(shift_of(c, tp), qq[c, tp].rearrange("p (a n b) -> p n a b", a=2, b=2), AXY, ALU.max, negate=True)
 
         def turn(dst, src, start, stop):
             nc.tensor.matmul(dst, lhsT=src, rhs=ident[:], start=start, stop=stop, is_transpose=True)
@@ -186,7 +186,7 @@ def tile_picked_ysoftq_lse_p_kernel(tc, x_words, x_scales, w1, w2, w3, disc, rew
             for d in range(D):
                 turn(dst, ee[c, tp][:, d * P : (d + 1) * P], d == 0, d == D - 1)
 
-        cast_w(0, 0, 0, P, False)
+        cast_w(0, 0, 0, P, True)
         cast_w(0, 0, P, HALF, False)
         quant_w(0, 0, 0, P)
         quant_w(0, 0, P, HALF)
@@ -204,38 +204,40 @@ def tile_picked_ysoftq_lse_p_kernel(tc, x_words, x_scales, w1, w2, w3, disc, rew
         quant_h(1)
         product(0, 0, 1)
         product(1, 0, 1)
-        cast_w(1, 1, 0, P, True)
+        cast_w(1, 1, 0, P, False)
         cast_w(1, 1, P, HALF, True)
         late = sb("late", [P, 5, 512], F32, tag="raw11_1")
-        neg_top[0] = sb("neg_top0", [P, 2, 2, VH], F32)[:]
-        neg_top[1] = sb("neg_top1", [P, 2, 2, VH], F32)[:]
+        for tp in range(2):
+            neg_top[tp] = late[:, 3, tp * HALF : (tp + 1) * HALF].rearrange("p (c s v) -> p c s v", c=2, s=2)
         first_out(0, 1, late[:, 0])
         quant_w(0, 1, P, HALF)
         product(0, 1, 0)
         product(0, 1, 1)
         first_out(1, 0, late[:, 1])
         first_out(1, 1, late[:, 2])
-        qq_first = over("qq00", [P, 512], F32, 4 * HALF)
-        smaller(0, 0, qq_first[:], 0, VH)
-        smaller(0, 0, qq_first[:], VH, P)
-        open_values(0, 0, [4] * D)
-        largest(0, 0, 0, VH)
-        largest(0, 0, VH, P)
+        qq_first = sb("qq00", [P, P, D], F32, tag="raw11_0")
+        nc.vector.tensor_tensor(qq_first[:].rearrange("p n d -> p (n d)"), q_bank[1, 0, 0][:], qa_sb[0, 0], ALU.min)
         quant_w(1, 1, 0, HALF)
         product(1, 1, 0)
         product(1, 1, 1)
-        close_shift(0, 0, late[:, 3])
+        nc.vector.tensor_reduce(shift_of(0, 0), qq_first[:], AX, ALU.max, negate=True)
+        first_d = sb("first_d", [P, P, D], F32)
+        nc.gpsimd.tensor_tensor(first_d[:], qq_first[:], shift_of(0, 0).unsqueeze(2).to_broadcast([P, P, D]), ALU.add)
+        first_e = sb("first_e", [P, P, D], F32)
+        nc.scalar.activation(first_e[:], first_d[:], ACT.Exp, scale=2.0)
         smaller(0, 1, late[:, 4])
         open_values(0, 1, [6] * D)
-        smaller(1, 0, sb("qq10", [P, 512], F32)[:])
+        qq_third = sb("qq10", [P, 512], F32)
+        smaller(1, 0, qq_third[:], 0, VH)
         largest(0, 1)
         close_shift(0, 1, sb("ee01", [P, 512], F32)[:])
+        smaller(1, 0, qq_third[:], VH, P)
         open_values(1, 0, [0, 2, 7, 1])
 
-        half_disc = sb("half_disc", [P, 4], F32)
+        half_disc = sb("half_disc", [P, 4], F32, tag="first_d")
         nc.gpsimd.tensor_scalar(half_disc[:], disc_sb[:], 0.5, 0.0, ALU.mult, ALU.add)
         neg_disc = sb("neg_disc", [P, 4], F32)
-        nc.gpsimd.tensor_scalar(neg_disc[:], disc_sb[:], -1.0, 0.0, ALU.mult, ALU.add)
+        nc.gpsimd.tensor_scalar(neg_disc[:], half_disc[:], -2.0, 0.0, ALU.mult, ALU.add)
 
         qq[LAST] = sb("qq11", [P, 512], F32)
         last_q = qq[LAST][:].rearrange("p (s v d) -> p s v d", s=2, d=D)
@@ -256,11 +258,12 @@ def tile_picked_ysoftq_lse_p_kernel(tc, x_words, x_scales, w1, w2, w3, disc, rew
             nc.vector.tensor_tensor(last_d[:, s], last_q[:, s], neg_top[1][:, 1, s, :].unsqueeze(2).to_broadcast([P, VH, D]), ALU.add)
             nc.scalar.activation(last_e[:, s], last_d[:, s], ACT.Exp, scale=2.0)
 
-        sums_first = bank(5)
-        sums_second = bank(4)
-        sum_back(0, 0, sums_first[:, 0:P])
+        sums_first = bank(2)
+        sums_second = bank(0)
         sum_back(0, 1, sums_second[:, 0:P])
-        sum_back(1, 0, sums_first[:, P : 2 * P])
+        sum_back(1, 0, sums_first[:, 0:P])
+        sums_early = qq[LAST][:, 0:P]
+        nc.vector.tensor_reduce(sums_early, first_e[:], AX, ALU.add)
 
         base = [qq[LAST][:, HALF:].rearrange("p (c s v) -> p c s v", c=2, s=2), neg_top[1]]
         for tt in range(4):
@@ -281,7 +284,7 @@ def tile_picked_ysoftq_lse_p_kernel(tc, x_words, x_scales, w1, w2, w3, disc, rew
             nc.scalar.activation(logs[1][:, 0, s, :], sums_second[:, s * VH : (s + 1) * VH], ACT.Ln)
             nc.scalar.activation(logs[1][:, 1, s, :], sums_last[:, s * VH : (s + 1) * VH], ACT.Ln)
             finish(2 + s)
-        first = sums_first[:, 0 : 2 * P].rearrange("p (c s v) -> p c s v", c=2, s=2)
+        nc.scalar.activation(logs[0][:, 0].rearrange("p s v -> p (s v)"), sums_early, ACT.Ln)
         for s in range(2):
-            nc.scalar.activation(logs[0][:, :, s, :], first[:, :, s, :], ACT.Ln)
+            nc.scalar.activation(logs[0][:, 1, s, :], sums_first[:, s * VH : (s + 1) * VH], ACT.Ln)
             finish(s)

@@ -44,7 +44,7 @@ def tile_picked_ysoftq_lse_p_kernel(tc, x_words, x_scales, w1, w2, w3, disc, rew
         offsets = keep.tile([P, S // 16], U16, name="offsets")
         xs = sb("xs", [P, T], U8)
         xw = sb("xw", [P, T], I32)
-        w1_raw = sb("w1_raw", [P, PACK, H], F32)
+        w1_raw = [sb(f"w1_raw{u}", [P, 2, H], F32) for u in range(2)]
 
         nc.vector.memset(xs[:].bitcast(I32), 0)
         early = sb("early", [P, 16], F32)
@@ -54,12 +54,12 @@ def tile_picked_ysoftq_lse_p_kernel(tc, x_words, x_scales, w1, w2, w3, disc, rew
         make_identity(nc, ident[:])
 
         w1_rows = w1.rearrange("(p j) c -> p j c", j=PACK)
-        nc.sync.dma_start(w1_raw[:, 0:2, :], w1_rows[:, 0:2, :])
+        nc.sync.dma_start(w1_raw[0][:], w1_rows[:, 0:2, :])
         nc.sync.dma_start(offsets[:], offs)
         x_flat = x_words[0].rearrange("p n t -> p (n t)").bitcast(I32)
         for r in range(4):
             nc.sync.dma_start(xs[r:P:32, :].bitcast(I32), x_scales[0, r:16:4, :].bitcast(I32))
-        nc.sync.dma_start(w1_raw[:, 2:4, :], w1_rows[:, 2:4, :])
+        nc.sync.dma_start(w1_raw[1][:], w1_rows[:, 2:4, :])
         nc.sync.dma_start(xw[:], x_flat)
         raw = {}
         for c in range(2):
@@ -81,8 +81,8 @@ def tile_picked_ysoftq_lse_p_kernel(tc, x_words, x_scales, w1, w2, w3, disc, rew
         nc.vector.tensor_copy(xs_g[:], xs[:].indirect(offsets[:]))
 
         w1_bf = sb("w1_bf", [P, PACK, P, PACK], BF16)
-        for lo, hi, copy in ((0, 84, nc.vector.tensor_copy), (84, P, nc.scalar.copy)):
-            copy(w1_bf[:, :, lo:hi, :].rearrange("p i m j -> p m i j"), w1_raw[:, :, PACK * lo : PACK * hi].rearrange("p j (m i) -> p m i j", i=PACK))
+        for u, lo, hi, copy in ((0, 0, P, nc.scalar.copy), (1, 0, 88, nc.vector.tensor_copy), (1, 88, P, nc.scalar.copy)):
+            copy(w1_bf[:, :, lo:hi, 2 * u : 2 * u + 2].rearrange("p i m j -> p m i j"), w1_raw[u][:, :, PACK * lo : PACK * hi].rearrange("p j (m i) -> p m i j", i=PACK))
         w1_c = sb("w1_c", [P, H], U32)
         w1_s = sb("w1_s", [P, H], U8)
         nc.vector.quantize_mx(w1_c[:].bitcast(FP8X4), w1_s[:], w1_bf[:].rearrange("p i m j -> p (i m j)"))

@@ -62,15 +62,14 @@ def tile_picked_ysoftq_lse_p_kernel(tc, x_words, x_scales, w1, w2, w3, disc, rew
         nc.sync.dma_start(w1_raw[1][:], w1_rows[:, 2:4, :])
         nc.sync.dma_start(xw[:], x_flat)
         raw = {}
-        for c in range(2):
-            for i, w in enumerate((w2, w3)):
-                if i == c:
-                    raw[i, c] = [sb(f"raw{i}{c}_{u}", [P, PACK, P], F32) for u in range(2)]
-                    for u in range(2):
-                        nc.sync.dma_start(raw[i, c][u][:], w.rearrange("(p j) c -> p j c", j=PACK)[:, :, c * HALF + u * P : c * HALF + (u + 1) * P])
-                    continue
-                raw[i, c] = over("raw01", [P, PACK, HALF], F32, 0) if (i, c) == (0, 1) else sb(f"raw{i}{c}", [P, PACK, HALF], F32)
-                nc.sync.dma_start(raw[i, c][:], w.rearrange("(p j) c -> p j c", j=PACK)[:, :, c * HALF : (c + 1) * HALF])
+        rows = [w.rearrange("(p j) c -> p j c", j=PACK) for w in (w2, w3)]
+        raw[0, 0] = [sb(f"raw00_{u}", [P, PACK, P], F32) for u in range(2)]
+        raw[1, 0] = sb("raw10", [P, PACK, HALF], F32)
+        raw[0, 1] = over("raw01", [P, PACK, HALF], F32, 0)
+        raw[1, 1] = [sb(f"raw11_{u}", [P, PACK, P], F32) for u in range(2)]
+        for dst, i, lo, hi in ((raw[0, 0][0], 0, 0, P), (raw[1, 0], 1, 0, HALF), (raw[0, 0][1], 0, P, HALF), (raw[0, 1], 0, HALF, G),
+                               (raw[1, 1][0], 1, HALF, HALF + P), (raw[1, 1][1], 1, HALF + P, G)):
+            nc.sync.dma_start(dst[:], rows[i][:, :, lo:hi])
         disc_sb = sb("disc_sb", [P, 4], F32)
         rew_sb = sb("rew_sb", [P, 4], F32)
         with nc.allow_non_contiguous_dma(reason="one value for each transition"):
@@ -81,15 +80,16 @@ def tile_picked_ysoftq_lse_p_kernel(tc, x_words, x_scales, w1, w2, w3, disc, rew
         nc.vector.tensor_copy(xs_g[:], xs[:].indirect(offsets[:]))
 
         w1_bf = sb("w1_bf", [P, PACK, P, PACK], BF16)
-        for u, lo, hi, copy in ((0, 0, P, nc.scalar.copy), (1, 0, 88, nc.vector.tensor_copy), (1, 88, P, nc.scalar.copy)):
+        for u, lo, hi, copy in ((0, 40, P, nc.scalar.copy), (0, 0, 40, nc.vector.tensor_copy), (1, 0, 88, nc.vector.tensor_copy), (1, 88, P, nc.scalar.copy)):
             copy(w1_bf[:, :, lo:hi, 2 * u : 2 * u + 2].rearrange("p i m j -> p m i j"), w1_raw[u][:, :, PACK * lo : PACK * hi].rearrange("p j (m i) -> p m i j", i=PACK))
         w1_c = sb("w1_c", [P, H], U32)
         w1_s = sb("w1_s", [P, H], U8)
-        nc.vector.quantize_mx(w1_c[:].bitcast(FP8X4), w1_s[:], w1_bf[:].rearrange("p i m j -> p (i m j)"))
+        for u in range(2):
+            nc.vector.quantize_mx(w1_c[:, u * HALF : (u + 1) * HALF].bitcast(FP8X4), w1_s[:, u * HALF : (u + 1) * HALF], w1_bf[:, 2 * u : 2 * u + 2].rearrange("p i m j -> p (i m j)"))
 
         warm = bank(7)
-        for r in range(2):
-            nc.tensor.matmul_mx(warm[:], lhsT=w1_c[:, 0:P].bitcast(FP8X4), lhsT_scale=w1_s[:, 0:P], rhs=w1_c[:].bitcast(FP8X4), rhs_scale=w1_s[:], start=True, stop=True)
+        for r in range(4):
+            nc.tensor.matmul_mx(warm[:, 0:HALF], lhsT=w1_c[:, 0:P].bitcast(FP8X4), lhsT_scale=w1_s[:, 0:P], rhs=w1_c[:, 0:HALF].bitcast(FP8X4), rhs_scale=w1_s[:, 0:HALF], start=True, stop=True)
 
         xw_g = []
         for half in range(2):
@@ -127,7 +127,7 @@ def tile_picked_ysoftq_lse_p_kernel(tc, x_words, x_scales, w1, w2, w3, disc, rew
             nc.vector.quantize_mx(w_c[i, c][:, lo:hi].bitcast(FP8X4), w_s[i, c][:, lo:hi], w_bf[i, c][:, lo:hi, :].rearrange("p n j -> p (n j)"))
 
         def quant_h(tp):
-            h_c[tp] = over("h_c1", [P, HALF], U32, 0) if tp else sb("h_c0", [P, HALF], U32, tag="raw10")
+            h_c[tp] = over("h_c1", [P, HALF], U32, 0) if tp else sb("h_c0", [P, HALF], U32, tag="raw00_1")
             h_s[tp] = sb(f"h_s{tp}", [P, HALF], U8)
             nc.vector.quantize_mx(h_c[tp][:].bitcast(FP8X4), h_s[tp][:], h_bf[tp][:].rearrange("p s n j -> p (s n j)"))
 
@@ -187,14 +187,12 @@ def tile_picked_ysoftq_lse_p_kernel(tc, x_words, x_scales, w1, w2, w3, disc, rew
                 turn(dst, ee[c, tp][:, d * P : (d + 1) * P], d == 0, d == D - 1)
 
         cast_w(0, 0, 0, P, True)
-        cast_w(0, 0, P, HALF, False)
         quant_w(0, 0, 0, P)
+        cast_w(1, 0, 0, HALF, False)
+        cast_w(0, 0, P, HALF, False)
+        quant_w(1, 0, 0, HALF)
         quant_w(0, 0, P, HALF)
-        cast_w(1, 0, 0, P, False)
-        cast_w(1, 0, P, HALF, False)
-        quant_w(1, 0, 0, P)
         quant_h(0)
-        quant_w(1, 0, P, HALF)
         product(0, 0, 0)
         product(1, 0, 0)
         first_out(0, 0, sb("qa00", [P, 512], F32)[:])

@@ -186,12 +186,11 @@ def tile_picked_ysoftq_lse_p_kernel(tc, x_words, x_scales, w1, w2, w3, disc, rew
             for d in range(D):
                 turn(dst, ee[c, tp][:, d * P : (d + 1) * P], d == 0, d == D - 1)
 
-        cast_w(0, 0, 0, P, True)
-        quant_w(0, 0, 0, P)
+        cast_w(0, 0, 0, P, False)
         cast_w(1, 0, 0, HALF, False)
         cast_w(0, 0, P, HALF, False)
         quant_w(1, 0, 0, HALF)
-        quant_w(0, 0, P, HALF)
+        quant_w(0, 0, 0, HALF)
         quant_h(0)
         product(0, 0, 0)
         product(1, 0, 0)

@@ -225,11 +225,10 @@ def tile_picked_ysoftq_lse_p_kernel(tc, x_words, x_scales, w1, w2, w3, disc, rew
         smaller(0, 1, late[:, 4])
         open_values(0, 1, [6] * D)
         qq_third = sb("qq10", [P, 512], F32)
-        smaller(1, 0, qq_third[:], 0, VH)
+        smaller(1, 0, qq_third[:])
+        open_values(1, 0, [0, 2, 7, 1])
         largest(0, 1)
         close_shift(0, 1, sb("ee01", [P, 512], F32)[:])
-        smaller(1, 0, qq_third[:], VH, P)
-        open_values(1, 0, [0, 2, 7, 1])
 
         half_disc = sb("half_disc", [P, 4], F32, tag="first_d")
         nc.gpsimd.tensor_scalar(half_disc[:], disc_sb[:], 0.5, 0.0, ALU.mult, ALU.add)
@@ -262,14 +261,14 @@ def tile_picked_ysoftq_lse_p_kernel(tc, x_words, x_scales, w1, w2, w3, disc, rew
         sums_early = qq[LAST][:, 0:P]
         nc.vector.tensor_reduce(sums_early, first_e[:], AX, ALU.add)
 
-        base = [qq[LAST][:, HALF:].rearrange("p (c s v) -> p c s v", c=2, s=2), neg_top[1]]
-        for tt in range(4):
-            tp, s = divmod(tt, 2)
-            nc.vector.tensor_scalar(base[tp][:, :, s, :], neg_top[tp][:, :, s, :], neg_disc[:, tt : tt + 1], rew_sb[:, tt : tt + 1], ALU.mult, ALU.add)
         sums_last = sb("sums_last", [P, 2 * VH], F32)
         nc.vector.tensor_reduce(sums_last[:], last_e[:].rearrange("p s v d -> p (s v) d"), AX, ALU.add)
+        base = [qq[LAST][:, HALF:].rearrange("p (c s v) -> p c s v", c=2, s=2), neg_top[1]]
+        for tt in (2, 3, 0, 1):
+            tp, s = divmod(tt, 2)
+            nc.vector.tensor_scalar(base[tp][:, :, s, :], neg_top[tp][:, :, s, :], neg_disc[:, tt : tt + 1], rew_sb[:, tt : tt + 1], ALU.mult, ALU.add)
 
-        logs = [t[:, 1].rearrange("p v d -> p (v d)").rearrange("p (c s v) -> p c s v", c=2, s=2) for t in (last_e, last_d)]
+        logs = [last_e[:, tp].rearrange("p v d -> p (v d)").rearrange("p (c s v) -> p c s v", c=2, s=2) for tp in range(2)]
 
         def finish(tt):
             tp, s = divmod(tt, 2)
@@ -278,8 +277,8 @@ def tile_picked_ysoftq_lse_p_kernel(tc, x_words, x_scales, w1, w2, w3, disc, rew
             nc.sync.dma_start(out[tt * P : (tt + 1) * P, :], res[:].rearrange("p c v -> p (c v)"))
 
         for s in range(2):
-            nc.scalar.activation(logs[1][:, 0, s, :], sums_second[:, s * VH : (s + 1) * VH], ACT.Ln)
             nc.scalar.activation(logs[1][:, 1, s, :], sums_last[:, s * VH : (s + 1) * VH], ACT.Ln)
+            nc.scalar.activation(logs[1][:, 0, s, :], sums_second[:, s * VH : (s + 1) * VH], ACT.Ln)
             finish(2 + s)
         nc.scalar.activation(logs[0][:, 0].rearrange("p s v -> p (s v)"), sums_early, ACT.Ln)
         for s in range(2):

@@ -20,26 +20,30 @@ ACT = mybir.ActivationFunctionType
 
 P = 128
 PACK = 4
+BANK = 512
 HALF = 256
-V = G // D
 VH = HALF // D
+QUADRANT = 32
+
+W1_GROUPS_ON_VECTOR = (40, 88)
+WARM_UP_PASSES = 4
 
 
 def tile_picked_ysoftq_lse_p_kernel(tc, x_words, x_scales, w1, w2, w3, disc, rew, offs, out):
     nc = tc.nc
     with ExitStack() as ctx:
         keep = ctx.enter_context(tc.tile_pool(name="keep", bufs=1))
-        shared = ctx.enter_context(tc.tile_pool(name="shared", bufs=1))
+        placed = ctx.enter_context(tc.tile_pool(name="placed", bufs=1))
         psum = ctx.enter_context(tc.psum_pool(name="psum", bufs=1))
 
         def sb(name, shape, dtype, tag=None):
             return keep.tile(shape, dtype, name=name, tag=tag or name, align_bytes=64)
 
-        def over(name, shape, dtype, offset):
-            return shared.tile(shape, dtype, name=name, offset=offset, align_bytes=64)
+        def sb_at(name, shape, dtype, offset):
+            return placed.tile(shape, dtype, name=name, offset=offset, align_bytes=64)
 
         def bank(b):
-            return psum.tile([P, 512], F32, name=f"bank{b}")
+            return psum.tile([P, BANK], F32, name=f"bank{b}")
 
         offsets = keep.tile([P, S // 16], U16, name="offsets")
         xs = sb("xs", [P, T], U8)
@@ -48,7 +52,7 @@ def tile_picked_ysoftq_lse_p_kernel(tc, x_words, x_scales, w1, w2, w3, disc, rew
 
         nc.vector.memset(xs[:].bitcast(I32), 0)
         early = sb("early", [P, 16], F32)
-        nc.gpsimd.memset(early[:, 0:8], 0.0)
+        nc.gpsimd.memset(early[:, 0:1], 0.0)
         nc.scalar.activation(early[:, 8:9], early[:, 0:1], ACT.Exp)
         ident = sb("ident", [P, P], F32)
         make_identity(nc, ident[:])
@@ -58,18 +62,24 @@ def tile_picked_ysoftq_lse_p_kernel(tc, x_words, x_scales, w1, w2, w3, disc, rew
         nc.sync.dma_start(offsets[:], offs)
         x_flat = x_words[0].rearrange("p n t -> p (n t)").bitcast(I32)
         for r in range(4):
-            nc.sync.dma_start(xs[r:P:32, :].bitcast(I32), x_scales[0, r:16:4, :].bitcast(I32))
+            nc.sync.dma_start(xs[r:P:QUADRANT, :].bitcast(I32), x_scales[0, r:16:4, :].bitcast(I32))
         nc.sync.dma_start(w1_raw[1][:], w1_rows[:, 2:4, :])
         nc.sync.dma_start(xw[:], x_flat)
         raw = {}
-        rows = [w.rearrange("(p j) c -> p j c", j=PACK) for w in (w2, w3)]
+        w_rows = [w.rearrange("(p j) c -> p j c", j=PACK) for w in (w2, w3)]
         raw[0, 0] = [sb(f"raw00_{u}", [P, PACK, P], F32) for u in range(2)]
         raw[1, 0] = sb("raw10", [P, PACK, HALF], F32)
-        raw[0, 1] = over("raw01", [P, PACK, HALF], F32, 0)
+        raw[0, 1] = sb_at("raw01", [P, PACK, HALF], F32, 0)
         raw[1, 1] = [sb(f"raw11_{u}", [P, PACK, P], F32) for u in range(2)]
-        for dst, i, lo, hi in ((raw[0, 0][0], 0, 0, P), (raw[1, 0], 1, 0, HALF), (raw[0, 0][1], 0, P, HALF), (raw[0, 1], 0, HALF, G),
-                               (raw[1, 1][0], 1, HALF, HALF + P), (raw[1, 1][1], 1, HALF + P, G)):
-            nc.sync.dma_start(dst[:], rows[i][:, :, lo:hi])
+        for dst, i, lo, hi in (
+            (raw[0, 0][0], 0, 0, P),
+            (raw[1, 0], 1, 0, HALF),
+            (raw[0, 0][1], 0, P, HALF),
+            (raw[0, 1], 0, HALF, G),
+            (raw[1, 1][0], 1, HALF, HALF + P),
+            (raw[1, 1][1], 1, HALF + P, G),
+        ):
+            nc.sync.dma_start(dst[:], w_rows[i][:, :, lo:hi])
         disc_sb = sb("disc_sb", [P, 4], F32)
         rew_sb = sb("rew_sb", [P, 4], F32)
         with nc.allow_non_contiguous_dma(reason="one value for each transition"):
@@ -80,45 +90,65 @@ def tile_picked_ysoftq_lse_p_kernel(tc, x_words, x_scales, w1, w2, w3, disc, rew
         nc.vector.tensor_copy(xs_g[:], xs[:].indirect(offsets[:]))
 
         w1_bf = sb("w1_bf", [P, PACK, P, PACK], BF16)
-        for u, lo, hi, copy in ((0, 40, P, nc.scalar.copy), (0, 0, 40, nc.vector.tensor_copy), (1, 0, 88, nc.vector.tensor_copy), (1, 88, P, nc.scalar.copy)):
-            copy(w1_bf[:, :, lo:hi, 2 * u : 2 * u + 2].rearrange("p i m j -> p m i j"), w1_raw[u][:, :, PACK * lo : PACK * hi].rearrange("p j (m i) -> p m i j", i=PACK))
+
+        def round_w1(u, lo, hi, copy):
+            copy(
+                w1_bf[:, :, lo:hi, 2 * u : 2 * u + 2].rearrange("p i m j -> p m i j"),
+                w1_raw[u][:, :, PACK * lo : PACK * hi].rearrange("p j (m i) -> p m i j", i=PACK),
+            )
+
+        round_w1(0, W1_GROUPS_ON_VECTOR[0], P, nc.scalar.copy)
+        round_w1(0, 0, W1_GROUPS_ON_VECTOR[0], nc.vector.tensor_copy)
+        round_w1(1, 0, W1_GROUPS_ON_VECTOR[1], nc.vector.tensor_copy)
+        round_w1(1, W1_GROUPS_ON_VECTOR[1], P, nc.scalar.copy)
         w1_c = sb("w1_c", [P, H], U32)
         w1_s = sb("w1_s", [P, H], U8)
         for u in range(2):
-            nc.vector.quantize_mx(w1_c[:, u * HALF : (u + 1) * HALF].bitcast(FP8X4), w1_s[:, u * HALF : (u + 1) * HALF], w1_bf[:, 2 * u : 2 * u + 2].rearrange("p i m j -> p (i m j)"))
+            cols = slice(u * HALF, (u + 1) * HALF)
+            nc.vector.quantize_mx(w1_c[:, cols].bitcast(FP8X4), w1_s[:, cols], w1_bf[:, 2 * u : 2 * u + 2].rearrange("p i m j -> p (i m j)"))
 
         warm = bank(7)
-        for r in range(4):
-            nc.tensor.matmul_mx(warm[:, 0:HALF], lhsT=w1_c[:, 0:P].bitcast(FP8X4), lhsT_scale=w1_s[:, 0:P], rhs=w1_c[:, 0:HALF].bitcast(FP8X4), rhs_scale=w1_s[:, 0:HALF], start=True, stop=True)
+        for warm_pass in range(WARM_UP_PASSES):
+            nc.tensor.matmul_mx(
+                warm[:, 0:HALF],
+                lhsT=w1_c[:, 0:P].bitcast(FP8X4),
+                lhsT_scale=w1_s[:, 0:P],
+                rhs=w1_c[:, 0:HALF].bitcast(FP8X4),
+                rhs_scale=w1_s[:, 0:HALF],
+                start=True,
+                stop=True,
+            )
 
         xw_g = []
-        for half in range(2):
-            g = sb(f"xw_g{half}", [P, HALF], U32)
-            nc.vector.tensor_copy(g[:], xw[:].bitcast(U32).indirect(offsets[:, 16 * half : 16 * (half + 1)]))
-            xw_g.append(g)
+        for tp in range(2):
+            picked = sb(f"xw_g{tp}", [P, HALF], U32)
+            nc.vector.tensor_copy(picked[:], xw[:].bitcast(U32).indirect(offsets[:, 16 * tp : 16 * (tp + 1)]))
+            xw_g.append(picked)
 
         h_bf = [sb(f"h_bf{tp}", [P, 2, P, PACK], BF16) for tp in range(2)]
         for tt in range(4):
-            hb = bank(tt)
-            cols = slice((tt % 2) * P, (tt % 2 + 1) * P)
+            tp, s = divmod(tt, 2)
+            h_bank = bank(tt)
             for i in range(PACK):
                 ch = slice(i * P, (i + 1) * P)
-                nc.tensor.matmul_mx(hb[:, ch], lhsT=w1_c[:, ch].bitcast(FP8X4), lhsT_scale=w1_s[:, ch],
-                                    rhs=xw_g[tt // 2][:, cols].bitcast(FP8X4), rhs_scale=xs_g[:, tt * P : (tt + 1) * P],
-                                    start=True, stop=True)
-            nc.scalar.activation(h_bf[tt // 2][:, tt % 2, :, :], hb[:].rearrange("p (i n) -> p n i", i=PACK), ACT.Relu)
+                nc.tensor.matmul_mx(
+                    h_bank[:, ch],
+                    lhsT=w1_c[:, ch].bitcast(FP8X4),
+                    lhsT_scale=w1_s[:, ch],
+                    rhs=xw_g[tp][:, s * P : (s + 1) * P].bitcast(FP8X4),
+                    rhs_scale=xs_g[:, tt * P : (tt + 1) * P],
+                    start=True,
+                    stop=True,
+                )
+            nc.scalar.activation(h_bf[tp][:, s, :, :], h_bank[:].rearrange("p (i n) -> p n i", i=PACK), ACT.Relu)
 
         w_bf, w_c, w_s, h_c, h_s = {}, {}, {}, {}, {}
 
-        def cast_w(i, c, lo, hi, on_scalar):
+        def round_w(i, c, lo, hi, copy):
             if (i, c) not in w_bf:
                 w_bf[i, c] = sb(f"w_bf{i}{c}", [P, HALF, PACK], BF16)
-            dst = w_bf[i, c][:, lo:hi, :].rearrange("p (n e) j -> p n j e", e=4)
-            src = (raw[i, c][lo // P][:] if i == c else raw[i, c][:, :, lo:hi]).rearrange("p j (n e) -> p n j e", e=4)
-            if on_scalar:
-                nc.scalar.copy(dst, src)
-            else:
-                nc.vector.tensor_copy(dst, src)
+            src = raw[i, c][lo // P][:] if isinstance(raw[i, c], list) else raw[i, c][:, :, lo:hi]
+            copy(w_bf[i, c][:, lo:hi, :].rearrange("p (n e) j -> p n j e", e=4), src.rearrange("p j (n e) -> p n j e", e=4))
 
         def quant_w(i, c, lo, hi):
             if (i, c) not in w_c:
@@ -126,15 +156,14 @@ def tile_picked_ysoftq_lse_p_kernel(tc, x_words, x_scales, w1, w2, w3, disc, rew
                 w_s[i, c] = sb(f"w_s{i}{c}", [P, HALF], U8)
             nc.vector.quantize_mx(w_c[i, c][:, lo:hi].bitcast(FP8X4), w_s[i, c][:, lo:hi], w_bf[i, c][:, lo:hi, :].rearrange("p n j -> p (n j)"))
 
-        def quant_h(tp):
-            h_c[tp] = over("h_c1", [P, HALF], U32, 0) if tp else sb("h_c0", [P, HALF], U32, tag="raw00_1")
+        def quant_h(tp, codes):
+            h_c[tp] = codes
             h_s[tp] = sb(f"h_s{tp}", [P, HALF], U8)
             nc.vector.quantize_mx(h_c[tp][:].bitcast(FP8X4), h_s[tp][:], h_bf[tp][:].rearrange("p s n j -> p (s n j)"))
 
-        LAST = (1, 1)
         qq, q_bank, qa_sb, neg_top, ee, diff = {}, {}, {}, {}, {}, {}
 
-        def read(bank_ap, c, tp):
+        def from_bank(bank_ap, c, tp):
             return bank_ap if c == tp else bank_ap.rearrange("p (n a b) -> p a n b", a=2, b=2)
 
         def laid(tile_ap, c, tp):
@@ -143,17 +172,24 @@ def tile_picked_ysoftq_lse_p_kernel(tc, x_words, x_scales, w1, w2, w3, disc, rew
         def product(i, c, tp):
             q_bank[i, c, tp] = bank(4 * (1 - c) + 2 * tp + i)
             for s in range(2):
-                rows = slice(s * P, (s + 1) * P)
-                nc.tensor.matmul_mx(q_bank[i, c, tp][:, s * HALF : (s + 1) * HALF], lhsT=h_c[tp][:, rows].bitcast(FP8X4), lhsT_scale=h_s[tp][:, rows],
-                                    rhs=w_c[i, c][:].bitcast(FP8X4), rhs_scale=w_s[i, c][:], start=True, stop=True)
+                tokens = slice(s * P, (s + 1) * P)
+                nc.tensor.matmul_mx(
+                    q_bank[i, c, tp][:, s * HALF : (s + 1) * HALF],
+                    lhsT=h_c[tp][:, tokens].bitcast(FP8X4),
+                    lhsT_scale=h_s[tp][:, tokens],
+                    rhs=w_c[i, c][:].bitcast(FP8X4),
+                    rhs_scale=w_s[i, c][:],
+                    start=True,
+                    stop=True,
+                )
 
-        def first_out(c, tp, dst):
+        def copy_out(c, tp, dst):
             qa_sb[c, tp] = dst
-            nc.scalar.copy(laid(dst, c, tp), read(q_bank[0, c, tp][:], c, tp))
+            nc.scalar.copy(laid(dst, c, tp), from_bank(q_bank[0, c, tp][:], c, tp))
 
-        def smaller(c, tp, dst, lo=0, hi=P):
+        def smaller(c, tp, dst):
             qq[c, tp] = dst
-            nc.vector.tensor_tensor(laid(dst, c, tp)[:, :, lo:hi], read(q_bank[1, c, tp][:], c, tp)[:, :, lo:hi], laid(qa_sb[c, tp], c, tp)[:, :, lo:hi], ALU.min)
+            nc.vector.tensor_tensor(laid(dst, c, tp), from_bank(q_bank[1, c, tp][:], c, tp), laid(qa_sb[c, tp], c, tp), ALU.min)
 
         def shift_of(c, tp):
             return neg_top[tp][:, c].rearrange("p s v -> p (s v)")
@@ -164,78 +200,81 @@ def tile_picked_ysoftq_lse_p_kernel(tc, x_words, x_scales, w1, w2, w3, disc, rew
         def turn(dst, src, start, stop):
             nc.tensor.matmul(dst, lhsT=src, rhs=ident[:], start=start, stop=stop, is_transpose=True)
 
-        def open_values(c, tp, banks):
+        def turn_values(c, tp, banks):
             tiles = {b: bank(b) for b in sorted(set(banks))}
             diff[c, tp] = [tiles[b] for b in banks]
             for d in range(D):
                 a, b = divmod(d, 2)
-                turn(diff[c, tp][d][:, d * P : (d + 1) * P], qq[c, tp][:, a * HALF + b : (a + 1) * HALF : 2], d == 0 or len(tiles) == D, False)
+                turn(diff[c, tp][d][:, d * P : (d + 1) * P], qq[c, tp][:, a * HALF + b : (a + 1) * HALF : 2], banks[d] not in banks[:d], False)
 
-        def close_shift(c, tp, dst):
+        def shift_and_exp(c, tp, banks, dst):
             ee[c, tp] = dst
-            apart = (c, tp) == (1, 0)
             for d in range(D):
-                cols = slice(d * P, (d + 1) * P)
-                turn(diff[c, tp][d][:, cols], shift_of(c, tp), False, apart or d == D - 1)
-                if apart:
+                closes = banks[d] not in banks[d + 1 :]
+                turn(diff[c, tp][d][:, d * P : (d + 1) * P], shift_of(c, tp), False, closes)
+                if closes:
+                    cols = slice(banks.index(banks[d]) * P, (d + 1) * P)
                     nc.scalar.activation(dst[:, cols], diff[c, tp][d][:, cols], ACT.Exp, scale=2.0)
-            if not apart:
-                nc.scalar.activation(dst, diff[c, tp][0][:], ACT.Exp, scale=2.0)
 
         def sum_back(c, tp, dst):
             for d in range(D):
                 turn(dst, ee[c, tp][:, d * P : (d + 1) * P], d == 0, d == D - 1)
 
-        cast_w(0, 0, 0, P, False)
-        cast_w(1, 0, 0, HALF, False)
-        cast_w(0, 0, P, HALF, False)
+        SECOND_BANKS = [6] * D
+        THIRD_BANKS = [0, 2, 7, 1]
+        LAST = (1, 1)
+
+        round_w(0, 0, 0, P, nc.vector.tensor_copy)
+        round_w(1, 0, 0, HALF, nc.vector.tensor_copy)
+        round_w(0, 0, P, HALF, nc.vector.tensor_copy)
         quant_w(1, 0, 0, HALF)
         quant_w(0, 0, 0, HALF)
-        quant_h(0)
+        quant_h(0, sb("h_c0", [P, HALF], U32, tag="raw00_1"))
         product(0, 0, 0)
         product(1, 0, 0)
-        first_out(0, 0, sb("qa00", [P, 512], F32)[:])
-        cast_w(0, 1, 0, P, False)
-        cast_w(0, 1, P, HALF, False)
+        copy_out(0, 0, sb("qa00", [P, BANK], F32)[:])
+        round_w(0, 1, 0, P, nc.vector.tensor_copy)
+        round_w(0, 1, P, HALF, nc.vector.tensor_copy)
         quant_w(0, 1, 0, P)
-        quant_h(1)
+        quant_h(1, sb_at("h_c1", [P, HALF], U32, 0))
         product(0, 0, 1)
         product(1, 0, 1)
-        cast_w(1, 1, 0, P, False)
-        cast_w(1, 1, P, HALF, True)
-        late = sb("late", [P, 5, 512], F32, tag="raw11_1")
+        quant_w(0, 1, P, HALF)
+        round_w(1, 1, 0, P, nc.vector.tensor_copy)
+        round_w(1, 1, P, HALF, nc.scalar.copy)
+        late = sb("late", [P, 5, BANK], F32, tag="raw11_1")
         for tp in range(2):
             neg_top[tp] = late[:, 3, tp * HALF : (tp + 1) * HALF].rearrange("p (c s v) -> p c s v", c=2, s=2)
-        first_out(0, 1, late[:, 0])
-        quant_w(0, 1, P, HALF)
+        copy_out(0, 1, late[:, 0])
         product(0, 1, 0)
         product(0, 1, 1)
-        first_out(1, 0, late[:, 1])
-        first_out(1, 1, late[:, 2])
-        qq_first = sb("qq00", [P, P, D], F32, tag="raw11_0")
-        nc.vector.tensor_tensor(qq_first[:].rearrange("p n d -> p (n d)"), q_bank[1, 0, 0][:], qa_sb[0, 0], ALU.min)
+        copy_out(1, 0, late[:, 1])
+        copy_out(1, 1, late[:, 2])
+        first_q = sb_at("qq00", [P, P, D], F32, HALF * 4)
+        smaller(0, 0, first_q[:].rearrange("p n d -> p (n d)"))
         quant_w(1, 1, 0, HALF)
         product(1, 1, 0)
         product(1, 1, 1)
-        nc.vector.tensor_reduce(shift_of(0, 0), qq_first[:], AX, ALU.max, negate=True)
+
+        nc.vector.tensor_reduce(shift_of(0, 0), first_q[:], AX, ALU.max, negate=True)
         first_d = sb("first_d", [P, P, D], F32)
-        nc.gpsimd.tensor_tensor(first_d[:], qq_first[:], shift_of(0, 0).unsqueeze(2).to_broadcast([P, P, D]), ALU.add)
+        nc.gpsimd.tensor_tensor(first_d[:], first_q[:], shift_of(0, 0).unsqueeze(2).to_broadcast([P, P, D]), ALU.add)
         first_e = sb("first_e", [P, P, D], F32)
         nc.scalar.activation(first_e[:], first_d[:], ACT.Exp, scale=2.0)
+
         smaller(0, 1, late[:, 4])
-        open_values(0, 1, [6] * D)
-        qq_third = sb("qq10", [P, 512], F32)
-        smaller(1, 0, qq_third[:])
-        open_values(1, 0, [0, 2, 7, 1])
+        turn_values(0, 1, SECOND_BANKS)
+        smaller(1, 0, sb("qq10", [P, BANK], F32)[:])
+        turn_values(1, 0, THIRD_BANKS)
         largest(0, 1)
-        close_shift(0, 1, sb("ee01", [P, 512], F32)[:])
+        shift_and_exp(0, 1, SECOND_BANKS, sb("ee01", [P, BANK], F32)[:])
 
         half_disc = sb("half_disc", [P, 4], F32, tag="first_d")
         nc.gpsimd.tensor_scalar(half_disc[:], disc_sb[:], 0.5, 0.0, ALU.mult, ALU.add)
         neg_disc = sb("neg_disc", [P, 4], F32)
         nc.gpsimd.tensor_scalar(neg_disc[:], half_disc[:], -2.0, 0.0, ALU.mult, ALU.add)
 
-        qq[LAST] = sb("qq11", [P, 512], F32)
+        qq[LAST] = sb("qq11", [P, BANK], F32)
         last_q = qq[LAST][:].rearrange("p (s v d) -> p s v d", s=2, d=D)
         last_d = sb("last_d", [P, 2, VH, D], F32)
         last_e = sb("last_e", [P, 2, VH, D], F32)
@@ -246,7 +285,7 @@ def tile_picked_ysoftq_lse_p_kernel(tc, x_words, x_scales, w1, w2, w3, disc, rew
 
         smaller_last(0)
         largest(1, 0)
-        close_shift(1, 0, sb("ee10", [P, 512], F32)[:])
+        shift_and_exp(1, 0, THIRD_BANKS, sb("ee10", [P, BANK], F32)[:])
         smaller_last(1)
         for s in range(2):
             nc.vector.tensor_reduce(neg_top[1][:, 1, s, :], last_q[:, s], AX, ALU.max, negate=True)
@@ -254,13 +293,12 @@ def tile_picked_ysoftq_lse_p_kernel(tc, x_words, x_scales, w1, w2, w3, disc, rew
             nc.vector.tensor_tensor(last_d[:, s], last_q[:, s], neg_top[1][:, 1, s, :].unsqueeze(2).to_broadcast([P, VH, D]), ALU.add)
             nc.scalar.activation(last_e[:, s], last_d[:, s], ACT.Exp, scale=2.0)
 
-        sums_first = bank(2)
+        sums_third = bank(2)
         sums_second = bank(0)
         sum_back(0, 1, sums_second[:, 0:P])
-        sum_back(1, 0, sums_first[:, 0:P])
-        sums_early = qq[LAST][:, 0:P]
-        nc.vector.tensor_reduce(sums_early, first_e[:], AX, ALU.add)
-
+        sum_back(1, 0, sums_third[:, 0:P])
+        sums_first = qq[LAST][:, 0:P]
+        nc.vector.tensor_reduce(sums_first, first_e[:], AX, ALU.add)
         sums_last = sb("sums_last", [P, 2 * VH], F32)
         nc.vector.tensor_reduce(sums_last[:], last_e[:].rearrange("p s v d -> p (s v) d"), AX, ALU.add)
         base = [qq[LAST][:, HALF:].rearrange("p (c s v) -> p c s v", c=2, s=2), neg_top[1]]
@@ -280,7 +318,7 @@ def tile_picked_ysoftq_lse_p_kernel(tc, x_words, x_scales, w1, w2, w3, disc, rew
             nc.scalar.activation(logs[1][:, 1, s, :], sums_last[:, s * VH : (s + 1) * VH], ACT.Ln)
             nc.scalar.activation(logs[1][:, 0, s, :], sums_second[:, s * VH : (s + 1) * VH], ACT.Ln)
             finish(2 + s)
-        nc.scalar.activation(logs[0][:, 0].rearrange("p s v -> p (s v)"), sums_early, ACT.Ln)
+        nc.scalar.activation(logs[0][:, 0].rearrange("p s v -> p (s v)"), sums_first, ACT.Ln)
         for s in range(2):
-            nc.scalar.activation(logs[0][:, 1, s, :], sums_first[:, s * VH : (s + 1) * VH], ACT.Ln)
+            nc.scalar.activation(logs[0][:, 1, s, :], sums_third[:, s * VH : (s + 1) * VH], ACT.Ln)
             finish(s)

from contextlib import ExitStack

import concourse.mybir as mybir
from concourse.masks import make_identity

K, T, S, H, D, G = 512, 2048, 512, 512, 4, 512
FLOPS = 2 * S * H * (K + 2 * G)

F32 = mybir.dt.float32
BF16 = mybir.dt.bfloat16
I32 = mybir.dt.int32
U32 = mybir.dt.uint32
U16 = mybir.dt.uint16
U8 = mybir.dt.uint8
FP8X4 = mybir.dt.float8_e4m3fn_x4
ALU = mybir.AluOpType
AX = mybir.AxisListType.X
AXY = mybir.AxisListType.XY
ACT = mybir.ActivationFunctionType

P = 128
PACK = 4
BANK = 512
HALF = 256
VH = HALF // D
QUADRANT = 32

W1_GROUPS_ON_VECTOR = (40, 88)
WARM_UP_PASSES = 4


def tile_picked_ysoftq_lse_p_kernel(tc, x_words, x_scales, w1, w2, w3, disc, rew, offs, out):
    nc = tc.nc
    with ExitStack() as ctx:
        keep = ctx.enter_context(tc.tile_pool(name="keep", bufs=1))
        placed = ctx.enter_context(tc.tile_pool(name="placed", bufs=1))
        psum = ctx.enter_context(tc.psum_pool(name="psum", bufs=1))

        def sb(name, shape, dtype, tag=None):
            return keep.tile(shape, dtype, name=name, tag=tag or name, align_bytes=64)

        def sb_at(name, shape, dtype, offset):
            return placed.tile(shape, dtype, name=name, offset=offset, align_bytes=64)

        def bank(b):
            return psum.tile([P, BANK], F32, name=f"bank{b}")

        offsets = keep.tile([P, S // 16], U16, name="offsets")
        xs = sb("xs", [P, T], U8)
        xw = sb("xw", [P, T], I32)
        w1_raw = [sb(f"w1_raw{u}", [P, 2, H], F32) for u in range(2)]

        nc.vector.memset(xs[:].bitcast(I32), 0)
        early = sb("early", [P, 16], F32)
        nc.gpsimd.memset(early[:, 0:1], 0.0)
        nc.scalar.activation(early[:, 8:9], early[:, 0:1], ACT.Exp)
        ident = sb("ident", [P, P], F32)
        make_identity(nc, ident[:])

        w1_rows = w1.rearrange("(p j) c -> p j c", j=PACK)
        nc.sync.dma_start(w1_raw[0][:], w1_rows[:, 0:2, :])
        nc.sync.dma_start(offsets[:], offs)
        x_flat = x_words[0].rearrange("p n t -> p (n t)").bitcast(I32)
        for r in range(4):
            nc.sync.dma_start(xs[r:P:QUADRANT, :].bitcast(I32), x_scales[0, r:16:4, :].bitcast(I32))
        nc.sync.dma_start(w1_raw[1][:], w1_rows[:, 2:4, :])
        nc.sync.dma_start(xw[:], x_flat)
        raw = {}
        w_rows = [w.rearrange("(p j) c -> p j c", j=PACK) for w in (w2, w3)]
        raw[0, 0] = [sb(f"raw00_{u}", [P, PACK, P], F32) for u in range(2)]
        raw[1, 0] = sb("raw10", [P, PACK, HALF], F32)
        raw[0, 1] = sb_at("raw01", [P, PACK, HALF], F32, 0)
        raw[1, 1] = [sb(f"raw11_{u}", [P, PACK, P], F32) for u in range(2)]
        for dst, i, lo, hi in (
            (raw[0, 0][0], 0, 0, P),
            (raw[1, 0], 1, 0, HALF),
            (raw[0, 0][1], 0, P, HALF),
            (raw[0, 1], 0, HALF, G),
            (raw[1, 1][0], 1, HALF, HALF + P),
            (raw[1, 1][1], 1, HALF + P, G),
        ):
            nc.sync.dma_start(dst[:], w_rows[i][:, :, lo:hi])
        disc_sb = sb("disc_sb", [P, 4], F32)
        rew_sb = sb("rew_sb", [P, 4], F32)
        with nc.allow_non_contiguous_dma(reason="one value for each transition"):
            nc.sync.dma_start(disc_sb[:], disc.rearrange("(s p) o -> p (s o)", p=P))
            nc.sync.dma_start(rew_sb[:], rew.rearrange("(s p) o -> p (s o)", p=P))

        xs_g = sb("xs_g", [P, S], U8)
        nc.vector.tensor_copy(xs_g[:], xs[:].indirect(offsets[:]))

        w1_bf = sb("w1_bf", [P, PACK, P, PACK], BF16)

        def round_w1(u, lo, hi, copy):
            copy(
                w1_bf[:, :, lo:hi, 2 * u : 2 * u + 2].rearrange("p i m j -> p m i j"),
                w1_raw[u][:, :, PACK * lo : PACK * hi].rearrange("p j (m i) -> p m i j", i=PACK),
            )

        round_w1(0, W1_GROUPS_ON_VECTOR[0], P, nc.scalar.copy)
        round_w1(0, 0, W1_GROUPS_ON_VECTOR[0], nc.vector.tensor_copy)
        round_w1(1, 0, W1_GROUPS_ON_VECTOR[1], nc.vector.tensor_copy)
        round_w1(1, W1_GROUPS_ON_VECTOR[1], P, nc.scalar.copy)
        w1_c = sb("w1_c", [P, H], U32)
        w1_s = sb("w1_s", [P, H], U8)
        for u in range(2):
            cols = slice(u * HALF, (u + 1) * HALF)
            nc.vector.quantize_mx(w1_c[:, cols].bitcast(FP8X4), w1_s[:, cols], w1_bf[:, 2 * u : 2 * u + 2].rearrange("p i m j -> p (i m j)"))

        warm = bank(7)
        for warm_pass in range(WARM_UP_PASSES):
            nc.tensor.matmul_mx(
                warm[:, 0:HALF],
                lhsT=w1_c[:, 0:P].bitcast(FP8X4),
                lhsT_scale=w1_s[:, 0:P],
                rhs=w1_c[:, 0:HALF].bitcast(FP8X4),
                rhs_scale=w1_s[:, 0:HALF],
                start=True,
                stop=True,
            )

        xw_g = []
        for tp in range(2):
            picked = sb(f"xw_g{tp}", [P, HALF], U32)
            nc.vector.tensor_copy(picked[:], xw[:].bitcast(U32).indirect(offsets[:, 16 * tp : 16 * (tp + 1)]))
            xw_g.append(picked)

        h_bf = [sb(f"h_bf{tp}", [P, 2, P, PACK], BF16) for tp in range(2)]
        for tt in range(4):
            tp, s = divmod(tt, 2)
            h_bank = bank(tt)
            for i in range(PACK):
                ch = slice(i * P, (i + 1) * P)
                nc.tensor.matmul_mx(
                    h_bank[:, ch],
                    lhsT=w1_c[:, ch].bitcast(FP8X4),
                    lhsT_scale=w1_s[:, ch],
                    rhs=xw_g[tp][:, s * P : (s + 1) * P].bitcast(FP8X4),
                    rhs_scale=xs_g[:, tt * P : (tt + 1) * P],
                    start=True,
                    stop=True,
                )
            nc.scalar.activation(h_bf[tp][:, s, :, :], h_bank[:].rearrange("p (i n) -> p n i", i=PACK), ACT.Relu)

        w_bf, w_c, w_s, h_c, h_s = {}, {}, {}, {}, {}

        def round_w(i, c, lo, hi, copy):
            if (i, c) not in w_bf:
                w_bf[i, c] = sb(f"w_bf{i}{c}", [P, HALF, PACK], BF16)
            src = raw[i, c][lo // P][:] if isinstance(raw[i, c], list) else raw[i, c][:, :, lo:hi]
            copy(w_bf[i, c][:, lo:hi, :].rearrange("p (n e) j -> p n j e", e=4), src.rearrange("p j (n e) -> p n j e", e=4))

        def quant_w(i, c, lo, hi):
            if (i, c) not in w_c:
                w_c[i, c] = sb(f"w_c{i}{c}", [P, HALF], U32)
                w_s[i, c] = sb(f"w_s{i}{c}", [P, HALF], U8)
            nc.vector.quantize_mx(w_c[i, c][:, lo:hi].bitcast(FP8X4), w_s[i, c][:, lo:hi], w_bf[i, c][:, lo:hi, :].rearrange("p n j -> p (n j)"))

        def quant_h(tp, codes):
            h_c[tp] = codes
            h_s[tp] = sb(f"h_s{tp}", [P, HALF], U8)
            nc.vector.quantize_mx(h_c[tp][:].bitcast(FP8X4), h_s[tp][:], h_bf[tp][:].rearrange("p s n j -> p (s n j)"))

        qq, q_bank, qa_sb, neg_top, ee, diff = {}, {}, {}, {}, {}, {}

        def from_bank(bank_ap, c, tp):
            return bank_ap if c == tp else bank_ap.rearrange("p (n a b) -> p a n b", a=2, b=2)

        def laid(tile_ap, c, tp):
            return tile_ap if c == tp else tile_ap.rearrange("p (a n b) -> p a n b", a=2, b=2)

        def product(i, c, tp):
            q_bank[i, c, tp] = bank(4 * (1 - c) + 2 * tp + i)
            for s in range(2):
                tokens = slice(s * P, (s + 1) * P)
                nc.tensor.matmul_mx(
                    q_bank[i, c, tp][:, s * HALF : (s + 1) * HALF],
                    lhsT=h_c[tp][:, tokens].bitcast(FP8X4),
                    lhsT_scale=h_s[tp][:, tokens],
                    rhs=w_c[i, c][:].bitcast(FP8X4),
                    rhs_scale=w_s[i, c][:],
                    start=True,
                    stop=True,
                )

        def copy_out(c, tp, dst):
            qa_sb[c, tp] = dst
            nc.scalar.copy(laid(dst, c, tp), from_bank(q_bank[0, c, tp][:], c, tp))

        def smaller(c, tp, dst):
            qq[c, tp] = dst
            nc.vector.tensor_tensor(laid(dst, c, tp), from_bank(q_bank[1, c, tp][:], c, tp), laid(qa_sb[c, tp], c, tp), ALU.min)

        def shift_of(c, tp):
            return neg_top[tp][:, c].rearrange("p s v -> p (s v)")

        def largest(c, tp):
            nc.vector.tensor_reduce(shift_of(c, tp), qq[c, tp].rearrange("p (a n b) -> p n a b", a=2, b=2), AXY, ALU.max, negate=True)

        def turn(dst, src, start, stop):
            nc.tensor.matmul(dst, lhsT=src, rhs=ident[:], start=start, stop=stop, is_transpose=True)

        def turn_values(c, tp, banks):
            tiles = {b: bank(b) for b in sorted(set(banks))}
            diff[c, tp] = [tiles[b] for b in banks]
            for d in range(D):
                a, b = divmod(d, 2)
                turn(diff[c, tp][d][:, d * P : (d + 1) * P], qq[c, tp][:, a * HALF + b : (a + 1) * HALF : 2], banks[d] not in banks[:d], False)

        def shift_and_exp(c, tp, banks, dst):
            ee[c, tp] = dst
            for d in range(D):
                closes = banks[d] not in banks[d + 1 :]
                turn(diff[c, tp][d][:, d * P : (d + 1) * P], shift_of(c, tp), False, closes)
                if closes:
                    cols = slice(banks.index(banks[d]) * P, (d + 1) * P)
                    nc.scalar.activation(dst[:, cols], diff[c, tp][d][:, cols], ACT.Exp, scale=2.0)

        def sum_back(c, tp, dst):
            for d in range(D):
                turn(dst, ee[c, tp][:, d * P : (d + 1) * P], d == 0, d == D - 1)

        SECOND_BANKS = [6] * D
        THIRD_BANKS = [0, 2, 7, 1]
        LAST = (1, 1)

        round_w(0, 0, 0, P, nc.vector.tensor_copy)
        round_w(1, 0, 0, HALF, nc.vector.tensor_copy)
        round_w(0, 0, P, HALF, nc.vector.tensor_copy)
        quant_w(1, 0, 0, HALF)
        quant_w(0, 0, 0, HALF)
        quant_h(0, sb("h_c0", [P, HALF], U32, tag="raw00_1"))
        product(0, 0, 0)
        product(1, 0, 0)
        copy_out(0, 0, sb("qa00", [P, BANK], F32)[:])
        round_w(0, 1, 0, P, nc.vector.tensor_copy)
        round_w(0, 1, P, HALF, nc.vector.tensor_copy)
        quant_w(0, 1, 0, P)
        quant_h(1, sb_at("h_c1", [P, HALF], U32, 0))
        product(0, 0, 1)
        product(1, 0, 1)
        quant_w(0, 1, P, HALF)
        round_w(1, 1, 0, P, nc.vector.tensor_copy)
        round_w(1, 1, P, HALF, nc.scalar.copy)
        late = sb("late", [P, 5, BANK], F32, tag="raw11_1")
        for tp in range(2):
            neg_top[tp] = late[:, 3, tp * HALF : (tp + 1) * HALF].rearrange("p (c s v) -> p c s v", c=2, s=2)
        copy_out(0, 1, late[:, 0])
        product(0, 1, 0)
        product(0, 1, 1)
        copy_out(1, 0, late[:, 1])
        copy_out(1, 1, late[:, 2])
        first_q = sb_at("qq00", [P, P, D], F32, HALF * 4)
        smaller(0, 0, first_q[:].rearrange("p n d -> p (n d)"))
        quant_w(1, 1, 0, HALF)
        product(1, 1, 0)
        product(1, 1, 1)

        nc.vector.tensor_reduce(shift_of(0, 0), first_q[:], AX, ALU.max, negate=True)
        first_d = sb("first_d", [P, P, D], F32)
        nc.gpsimd.tensor_tensor(first_d[:], first_q[:], shift_of(0, 0).unsqueeze(2).to_broadcast([P, P, D]), ALU.add)
        first_e = sb("first_e", [P, P, D], F32)
        nc.scalar.activation(first_e[:], first_d[:], ACT.Exp, scale=2.0)

        smaller(0, 1, late[:, 4])
        turn_values(0, 1, SECOND_BANKS)
        smaller(1, 0, sb("qq10", [P, BANK], F32)[:])
        turn_values(1, 0, THIRD_BANKS)
        largest(0, 1)
        shift_and_exp(0, 1, SECOND_BANKS, sb("ee01", [P, BANK], F32)[:])

        half_disc = sb("half_disc", [P, 4], F32, tag="first_d")
        nc.gpsimd.tensor_scalar(half_disc[:], disc_sb[:], 0.5, 0.0, ALU.mult, ALU.add)
        neg_disc = sb("neg_disc", [P, 4], F32)
        nc.gpsimd.tensor_scalar(neg_disc[:], half_disc[:], -2.0, 0.0, ALU.mult, ALU.add)

        qq[LAST] = sb("qq11", [P, BANK], F32)
        last_q = qq[LAST][:].rearrange("p (s v d) -> p s v d", s=2, d=D)
        last_d = sb("last_d", [P, 2, VH, D], F32)
        last_e = sb("last_e", [P, 2, VH, D], F32)

        def smaller_last(s):
            cols = slice(s * HALF, (s + 1) * HALF)
            nc.vector.tensor_tensor(qq[LAST][:, cols], q_bank[1, 1, 1][:, cols], qa_sb[LAST][:, cols], ALU.min)

        smaller_last(0)
        largest(1, 0)
        shift_and_exp(1, 0, THIRD_BANKS, sb("ee10", [P, BANK], F32)[:])
        smaller_last(1)
        for s in range(2):
            nc.vector.tensor_reduce(neg_top[1][:, 1, s, :], last_q[:, s], AX, ALU.max, negate=True)
        for s in range(2):
            nc.vector.tensor_tensor(last_d[:, s], last_q[:, s], neg_top[1][:, 1, s, :].unsqueeze(2).to_broadcast([P, VH, D]), ALU.add)
            nc.scalar.activation(last_e[:, s], last_d[:, s], ACT.Exp, scale=2.0)

        sums_third = bank(2)
        sums_second = bank(0)
        sum_back(0, 1, sums_second[:, 0:P])
        sum_back(1, 0, sums_third[:, 0:P])
        sums_first = qq[LAST][:, 0:P]
        nc.vector.tensor_reduce(sums_first, first_e[:], AX, ALU.add)
        sums_last = sb("sums_last", [P, 2 * VH], F32)
        nc.vector.tensor_reduce(sums_last[:], last_e[:].rearrange("p s v d -> p (s v) d"), AX, ALU.add)
        base = [qq[LAST][:, HALF:].rearrange("p (c s v) -> p c s v", c=2, s=2), neg_top[1]]
        for tt in (2, 3, 0, 1):
            tp, s = divmod(tt, 2)
            nc.vector.tensor_scalar(base[tp][:, :, s, :], neg_top[tp][:, :, s, :], neg_disc[:, tt : tt + 1], rew_sb[:, tt : tt + 1], ALU.mult, ALU.add)

        logs = [last_e[:, tp].rearrange("p v d -> p (v d)").rearrange("p (c s v) -> p c s v", c=2, s=2) for tp in range(2)]

        def finish(tt):
            tp, s = divmod(tt, 2)
            res = sb(f"res{tt}", [P, 2, VH], F32)
            nc.vector.scalar_tensor_tensor(res[:], logs[tp][:, :, s, :], half_disc[:, tt : tt + 1], base[tp][:, :, s, :], ALU.mult, ALU.add)
            nc.sync.dma_start(out[tt * P : (tt + 1) * P, :], res[:].rearrange("p c v -> p (c v)"))

        for s in range(2):
            nc.scalar.activation(logs[1][:, 1, s, :], sums_last[:, s * VH : (s + 1) * VH], ACT.Ln)
            nc.scalar.activation(logs[1][:, 0, s, :], sums_second[:, s * VH : (s + 1) * VH], ACT.Ln)
            finish(2 + s)
        nc.scalar.activation(logs[0][:, 0].rearrange("p s v -> p (s v)"), sums_first, ACT.Ln)
        for s in range(2):
            nc.scalar.activation(logs[0][:, 1, s, :], sums_third[:, s * VH : (s + 1) * VH], ACT.Ln)
            finish(s)
